import numpy as np, ml_dtypes
CORES = [16,17,18,19,32,33,34,35]
N = 8
BF = ml_dtypes.bfloat16
def gentries(a):
    return np.ascontiguousarray(a.reshape(8, 16, -1).transpose(0, 2, 1)).reshape(8, -1)
def gtable(e):
    e = np.asarray(e); return np.ascontiguousarray(e.reshape(8, -1, 16).transpose(0, 2, 1)).reshape(128, -1).astype(np.int32)
P, LG, I, K, M, RO = 4096, 12, 128, 64, 32, 3
RHO, KA, KB, LIGHT, HALF = 64, 3, 4, 48, 7168
def lists(rng):
    return np.argsort(rng.random((N, 8, 4, P)), axis=-1)
def parts(rng):
    x = rng.integers(0, 256, (N, 8, 16, P)); z = rng.integers(0, 256, (N, 8, 16, 4 * I))
    lev = rng.permuted(np.tile(np.array([0.95, 0.83, 0.74, 0.69, 0.65, 0.6, 0.53, 0.42]), (N, 1)), axis=1)
    w = np.minimum(rng.geometric(lev[:, :, None], (N, 8, P)), 8)
    return x, w, z, lists(rng)
def pack(x, w, z, mem):
    return {"pt": np.ascontiguousarray(x.reshape(N, 128, P)).astype(np.float32).astype(BF), "w0": np.ascontiguousarray(w).astype(np.float32).astype(BF),
            "z0": np.ascontiguousarray(z.reshape(N, 128, 4 * I)).astype(np.float32).astype(BF), "lm": np.stack([gtable(a.reshape(8, -1)) for a in mem])}
def total(rng, s):
    e = (s - P) >> 4; w = np.ones(P, np.int64); w[:e] = 8; w[e:e + s - P - 7 * e] = 2
    return rng.permutation(w)
def setup_inputs(rng):
    return pack(*parts(rng))
def setup_inputs_spread(rng):
    def uneven(n):
        v = np.floor(np.exp2(8 * rng.random((N, 8, 1, n))) * rng.random((N, 8, 16, n))).astype(np.int64)
        return np.where(rng.random(v.shape) < 0.5, v, 255 - v)
    x, z = uneven(P), uneven(4 * I)
    ex = rng.permuted(np.tile(np.array([1.0, 2.0, 3.0, 5.0, 8.0, 12.0, 16.0, 24.0]), (N, 1)), axis=1)
    w = 1 + np.minimum(np.floor(8 * rng.random((N, 8, P)) ** ex[:, :, None]).astype(np.int64), 7)
    return pack(x, w, z, lists(rng))
def setup_inputs_ends(rng):
    def two(n):
        e = 255 * rng.integers(0, 2, (N, 8, 16, n)); m = rng.integers(0, 7, (N, 8, 1, n))
        return np.where(m == 0, 0, np.where(m == 1, 255, e))
    x, z = two(P), two(4 * I); w = np.ones((N, 8, P), np.int64)
    s = rng.permuted(np.tile(np.array([0.02, 0.06, 0.1, 0.15, 0.3, 0.5]), (N, 1)), axis=1)
    w[:, 1:7] = np.where(rng.random((N, 6, P)) < s[:, :, None], 8, 1); w[:, 1:7, 0] = 8; w[:, 1:7, P - 1] = 8
    w[0::2, 0] = 8; w[1::2, 7] = 8
    z[:, 1:6:2, :, I - 1::I] = 255; z[:, 0:7:2, :, I - 1::I] = 0
    for r in (0, N - 1): x[r, 7] = 255 * (rng.random((16, P)) < 0.03125)
    z[0, 7] = 255; z[1, 7] = 255
    inner = np.arange(4 * I) % I < I - 1; coin = rng.random((2, 4 * I)) < 0.5
    z[0:2, 7, 7] = np.where(inner & coin, 254, 255); z[0:2, 7, 15] = np.where(inner & ~coin, 254, 255)
    h = np.arange(P >> 1); seq = np.stack([h, P - 1 - h], axis=1).reshape(I, M)
    lan = np.argsort(rng.random((N, 4, 4, I)), axis=-1)
    lan[:, :, 0] = np.concatenate([1 + np.argsort(rng.random((N, 4, I - 1)), axis=-1), np.zeros((N, 4, 1), np.int64)], axis=-1)
    mem = lists(rng); mem[:, 0::2] = seq[lan].reshape(N, 4, 4, P)
    return pack(x, w, z, mem)
def setup_inputs_corners(rng):
    x, w, z, mem = parts(rng); o = [int(a) for a in rng.permutation(8)]
    x[:, o[0]] = rng.integers(100, 101 + (RHO >> 1), (N, 16, P)); z[:, o[0]] = rng.integers(100, 101 + (RHO >> 1), (N, 16, 4 * I))
    b = rng.integers(110, 141, (1, 16, 1)); x[:, o[1]] = b
    n = rng.choice(np.array([11, 12, 13, 16]), (N, 1, 4 * I)); pl = np.argsort(rng.random((N, 16, 4 * I)), axis=1)
    z[:, o[1]] = b + np.where(pl < n, RHO, RHO + 1) * rng.choice(np.array([-1, 1]), (N, 16, 4 * I))
    x[:, o[2]] = rng.integers(200, 256, (N, 16, P)); z[:, o[2]] = rng.integers(0, 21, (N, 16, 4 * I))
    for r in range(N):
        w[r, o[0]] = total(rng, (HALF, HALF + 1, 2 * P, 2 * P - 1)[r % 4]); w[r, o[3]] = total(rng, (2 * P + 1, 2 * P, 2 * P - 1, P)[r % 4])
        k = rng.integers(0, 4, (I, 1)); k[:4, 0] = rng.permutation(4); k[I - 1, 0] = 1 + r % 2
        twos = np.where(k == 0, 0, np.where(k == 1, (M >> 1) - 1, M >> 1))
        v = np.where(k == 3, 8, np.where(np.arange(M)[None, :] < twos, 2, 1))
        w[r, o[2], mem[r, o[2], 0]] = v.reshape(-1)
    w[:, o[4]] = 8; w[:, o[5]] = 1; w[:, o[6]] = 1; w[:, o[6], :P >> 2] = 8
    m = rng.integers(0, 3, (N, 1, 4 * I)); z[:, o[7]] = np.where(m == 0, 0, np.where(m == 1, 255, z[:, o[7]]))
    return pack(x, w, z, mem)
def setup_inputs_crowd(rng):
    x, w, z, mem = parts(rng); o = [int(a) for a in rng.permutation(8)]
    j = o.index(7 - o[0]); o[j], o[7] = o[7], o[j]
    for g in o[:5]:
        x[:, g] = rng.integers(200, 256, (N, 16, P)); z[:, g] = rng.integers(0, 21, (N, 16, 4 * I))
    w[:, o[0]] = rng.integers(2, 9, (N, P)); w[:, o[1]] = rng.integers(2, 9, (N, P)); w[:, o[2]] = 1; w[:, o[3]] = 1
    for r in range(N):
        a = int(rng.integers(0, I)); a = I - 1 if r == 0 else 0 if r == 1 else a
        z[r, o[1], :, a::I] = 227
        a = int(rng.integers(0, I)); a = I - 1 if r == N - 1 else a
        w[r, o[3], mem[r, o[3], 0, a * M:(a + 1) * M]] = 8
    mem[:, o[4], 1] = mem[:, o[4], 0].reshape(N, -1, 2, M)[:, :, ::-1].reshape(N, P)
    z[:, o[4], :, 1:I:2] = 227; w[:, o[4]] = np.minimum(rng.geometric(0.9, (N, P)), 8)
    z[:, o[5]] = 0
    x[:, o[6]] = rng.integers(200, 256, (N, 16, P)); z[:, o[6]] = 227; w[:, o[6]] = 1
    for r in range(N):
        n = int(rng.integers(7 * I >> 4, (17 * I >> 5) + 1)); a = rng.permutation(I)[:n]
        zv = z[(r + 1) % N, o[6]]; zv[:, a] = rng.integers(0, 21, (16, n))
        wv = w[r, o[6]]; wv[mem[r, o[6], 0].reshape(I, M)[a, :M >> 4]] = 8
    x[:, o[7]] = rng.integers(200, 256, (N, 16, P)); z[:, o[7]] = rng.integers(0, 21, (N, 16, 4 * I)); w[:, o[7]] = rng.integers(2, 9, (N, P))
    z[:, o[7], :, :I] = 227; z[:, o[7], :, 2 * I:3 * I] = 227
    for r in range(1, N, 2):
        a = int(rng.integers(0, I)); a = I - 1 if r == N - 1 else 0 if r == 1 else a
        z[r, o[7], :, I + a] = 227
    return pack(x, w, z, mem)
def check_inputs(d):
    bad = []
    for k, lo, hi in (("pt", 0, 255), ("w0", 1, 8), ("z0", 0, 255), ("lm", 0, P - 1)):
        a = np.asarray(d[k]).astype(np.float64)
        if not np.all((a >= lo) & (a <= hi)): bad.append("range of " + k)
        if np.any(a != np.floor(a)): bad.append("whole numbers of " + k)
    e = np.sort(np.stack([gentries(a) for a in np.asarray(d["lm"])]).reshape(-1, P), axis=1)
    if np.any(e != np.arange(P)[None, :]): bad.append("lm: the members of a class are all different")
    return bad
def reference(pt, w0, z0, lm):
    x = pt.astype(np.float32).astype(np.int64).reshape(N, 8, 16, P); w = w0.astype(np.float32).astype(np.int64).reshape(N, 8, P)
    z = z0.astype(np.float32).astype(np.int64).reshape(N, 8, 16, 4 * I); mem = np.stack([gentries(a) for a in lm]).astype(np.int64).reshape(N, 8, 4, I, M)
    kap = KA + KB * np.arange(K); cof = 2 * np.arange(16) + 1
    A = np.zeros((N, 8), np.int64); tally = np.zeros((N, 8, RO), np.int64)
    for t in range(RO):
        c = (t % 4, (t + 1) % 4); zn = z.copy()
        for r in range(N):
            q = (r + 1 + t % (N - 1)) % N
            for g in range(8):
                zz = [z[q, g, :, a * I:(a + 1) * I] for a in c]
                wg = w[r, g].copy(); T = min(int(np.sum(wg)), 2 * P); E = np.repeat(np.arange(P), wg)[:T]
                u = np.dot(cof, zz[0])
                h = (((u[:, None] * kap[None, :]) >> 4) + 61 * np.arange(I)[:, None] + A[r, g]) & (P - 1)
                net = E[(h * (T >> 1)) >> (LG - 1)]
                p = x[r, g][:, net]
                miss = [~np.any(np.sum(np.abs(p - b[:, :, None]) <= RHO, axis=0) >= 12, axis=1) for b in zz]
                y = (np.max(p, axis=2) + np.min(p, axis=2)) >> 1
                mark = np.zeros(P, bool); heavy = 0
                for m in (0, 1):
                    sel = miss[0] if m == 0 else miss[1] & ~miss[0]
                    s = np.sum(wg[mem[r, g, c[m]]], axis=1); light = sel & (s < LIGHT)
                    mark[mem[r, g, c[m]][light]] = True; heavy = heavy + int(np.sum(sel & ~light))
                    zn[q, g, :, c[m] * I:(c[m] + 1) * I] = np.where(sel[None, :], (zz[m] + y) >> 1, zz[m])
                wg = np.where(mark, np.minimum(2 * wg, 8), wg)
                if int(np.sum(wg)) > HALF: wg = (wg + 1) >> 1
                w[r, g] = wg; A[r, g] = heavy; tally[r, g, t] = heavy
        z = zn
    return {"yw": w.astype(np.float32), "yz": z.reshape(N, 128, 4 * I).astype(np.float32).astype(BF), "ya": tally.astype(np.float32)}

@@ -1,0 +1,410 @@
+from concourse.mybir import AluOpType, AxisListType, ActivationFunctionType
+
+OP = AluOpType
+COPY = ActivationFunctionType.Copy
+OFF = 24576.0
+CH = 2048
+AW = CH + 16
+PSUM = ["pcs", "pex", "pu", "pt1", "pe0", "cnt0", "cnt1", "pc"]
+F, H, I32, U16, H16 = "float32", "bfloat16", "int32", "uint16", "float16"
+_SB = {
+    "ptb": (4096, H), "lmb": (1024, I32), "lf": (256, F), "ldiff": (256, F), "ph": (4096, H), "net": (4 * AW, H),
+    "sh": (CH, H16), "v0": (8192, H), "v1": (8192, H), "wr": (4096, H), "gg": (4096, H),
+    "wm": (16384, H), "we": (16384, H), "big": (4096, F),
+    "cb": (2048, H), "lw": (2048, H), "rb": (2048, H), "mxm": (CH, H), "mnm": (CH, H), "dm1": (CH, H),
+    "pidx": (4, I32), "col": (32, F), "xa": (256, F), "xg": (128, F), "dmk": (256, F), "bd": (128, H),
+    "sl": (128, H), "ul": (128, H), "b8": (128, H), "mc": (256, H), "clf": (16, F), "cl": (16, U16),
+    "i61": (512, F), "zer": (256, F), "seg": (256, H), "zs": (512, H), "zz0": (256, H), "zz1": (256, H), "zz2": (256, H),
+    "zf": (512, H), "dz": (256, H), "wl": (256, H), "w1": (256, H), "wi": (256, I32), "inc": (264, F), "ti": (8, I32),
+    "tc": (8, F), "db": (272, F), "msk": (256, F), "sg": (256, F), "ci": (272, I32), "p1": (272, F),
+    "hsb": (280, F), "offs": (16, U16), "dl": (256, F), "dlb": (256, H), "el": (256, U16), "hi": (512, I32), "hl": (512, U16),
+    "cm": (1024, H), "cx": (256, H), "m": (256, F), "t0": (256, F), "slf": (256, F), "so": (256, U16), "bm": (256, F),
+    "h1": (128, F), "hh": (128, F), "pen": (128, H), "selz": (256, F), "mk8": (128, F), "mo": (256, U16), "ab": (8, F),
+    "ys": (128, F), "y2": (256, I32), "q": (256, F), "qi": (256, I32), "zn0": (256, H), "zn1": (256, H), "zn2": (256, H),
+}
+SCRATCH = {k: ("sbuf", [128, n], d) for k, (n, d) in _SB.items()}
+for _k in PSUM:
+    SCRATCH[_k] = ("psum", [128, 512], "float32")
+NDMA = 14
+ARR = ["a01", "a2", "a3", "ac1", "ac2", "af0", "af1", "af2"]
+SEMAPHORES = ["sv", "ss", "st", "sg"] + ["d%d" % k for k in range(NDMA)] + ["l%d" % k for k in range(8)] + ARR
+
+
+def overlap(a, b):
+    if a[0] >= b[1] or b[0] >= a[1]:
+        return False
+    if a[2] == b[2] and a[2] > 1 and (a[0] - b[0]) % a[2]:
+        return False
+    return True
+
+
+def rank_program(g, core, T, topo):
+    rank = T.rank_of(core)
+    if rank is None:
+        return
+    N = len(T.cores)
+    queues = {"v": g.vector, "s": g.scalar, "t": g.tensor, "g": g, "y": g.sync}
+    csem = {"v": "sv", "s": "ss", "t": "st", "g": "sg"}
+    known = {e: {} for e in queues}
+    total = {}
+    hist = {}
+    ndma, nloc = [0], [0]
+
+    def regs(items):
+        out = []
+        for it in items:
+            if len(it) == 3: it = it + (1,)
+            out.append(it)
+        return out
+
+    def order(e, reads, writes, acc):
+        need = []
+        for mode, items in (("r", reads), ("w", writes)):
+            for (b, lo, hi, st) in items:
+                for (pm, pe, reg, tok) in hist.get(b, []):
+                    if b in PSUM and pe != e:
+                        need.append(tok)
+                        continue
+                    if mode == "r" and pm == "r": continue
+                    if acc and pe == e and mode == "w": continue
+                    if overlap((lo, hi, st), reg): need.append(tok)
+        todo = {}
+        for (s, v, clk) in need:
+            if known[e].get(s, 0) < v and (s not in todo or todo[s][0] < v):
+                todo[s] = (v, clk)
+        for s in sorted(todo, key=lambda x: -len(todo[x][1])):
+            v, clk = todo[s]
+            if known[e].get(s, 0) >= v: continue
+            if any(o != s and known[e].get(o, 0) < todo[o][0] and todo[o][1].get(s, 0) >= v for o in todo): continue
+            queues[e].wait_ge(T.sem[s], v)
+            for k, x in clk.items():
+                if known[e].get(k, 0) < x: known[e][k] = x
+            known[e][s] = v
+
+    def note(e, reads, writes, tok):
+        for (b, lo, hi, st) in writes:
+            keep = []
+            for h in hist.get(b, []):
+                r = h[2]
+                if st == 1 and lo <= r[0] and r[1] <= hi and b not in PSUM: continue
+                keep.append(h)
+            hist[b] = keep + [("w", e, (lo, hi, st), tok)]
+        for (b, lo, hi, st) in reads:
+            hist.setdefault(b, []).append(("r", e, (lo, hi, st), tok))
+
+    def do(e, fn, reads, writes, acc=False):
+        reads, writes = regs(reads), regs(writes)
+        order(e, reads, writes, acc)
+        s = csem[e]
+        total[s] = total.get(s, 0) + 1
+        fn(queues[e]).then_inc(T.sem[s], 1)
+        clk = dict(known[e]); clk[s] = total[s]
+        note(e, reads, writes, (s, total[s], clk))
+
+    def dma(e, out, in_, reads, writes):
+        reads, writes = regs(reads), regs(writes)
+        order(e, reads, writes, False)
+        s = "d%d" % ndma[0]; ndma[0] += 1
+        total[s] = 16
+        queues[e].dma_start(out=out, in_=in_).then_inc(T.sem[s], 16)
+        clk = dict(known[e]); clk[s] = 16
+        note("dma" + s, reads, writes, (s, 16, clk))
+
+    def send(dst_rank, buf, lo, hi, dbuf, dlo, rsem):
+        dst = T.cores[dst_rank % N]
+        order("g", [(buf, lo, hi, 1)], [], False)
+        eng = topo.engines(core, dst)[:8:2]
+        mask = sum(1 << x for x in eng)
+        s = "l%d" % nloc[0]; nloc[0] += 1
+        total[s] = len(eng)
+        rid, pid, _se = topo.addr(dst)
+        g.remote_dma(out_ap=T[dbuf][:, dlo:dlo + hi - lo], in_ap=T[buf][:, lo:hi], remote_sem=T.sem[rsem], local_sem=T.sem[s],
+                     pid=pid, routing_id=rid, dma_engine_mask=mask)
+        note("rem", [(buf, lo, hi, 1)], [], (s, len(eng), {s: len(eng)}))
+
+    def arrives(src_rank, buf, lo, hi, rsem):
+        n = len(topo.engines(T.cores[src_rank % N], core)[:8:2])
+        total[rsem] = n
+        note("arr", [], [(buf, lo, hi, 1)], (rsem, n, {rsem: n}))
+
+    def A(x):
+        return T[x[0]][:, x[1]:x[2]] if len(x) == 3 else T[x[0]][:, x[1]:x[2]:x[3]]
+
+    def isc(x): return not isinstance(x, (int, float))
+
+    def cp(out, in_): do("v", lambda q: q.tensor_copy(out=A(out), in_=A(in_)), [in_], [out])
+    def tt(out, a, b, op): do("v", lambda q: q.tensor_tensor(out=A(out), in0=A(a), in1=A(b), op=op), [a, b], [out])
+
+    def ts(out, a, s1, op0, s2=None, op1=None):
+        rd = [a] + [s for s in (s1, s2) if s is not None and isc(s)]
+        x1 = A(s1) if isc(s1) else s1
+        x2 = A(s2) if s2 is not None and isc(s2) else s2
+        if op1 is None: do("v", lambda q: q.tensor_scalar(out=A(out), in0=A(a), scalar1=x1, scalar2=None, op0=op0), rd, [out])
+        else: do("v", lambda q: q.tensor_scalar(out=A(out), in0=A(a), scalar1=x1, scalar2=x2, op0=op0, op1=op1), rd, [out])
+
+    def scan(out, d0, d1, init, op0, op1):
+        rd = [d0, d1] + ([init] if isc(init) else [])
+        x = A(init) if isc(init) else init
+        do("v", lambda q: q.tensor_tensor_scan(A(out), A(d0), A(d1), x, op0, op1), rd, [out])
+
+    def fill(out, c): do("v", lambda q: q.memset(A(out), c), [], [out])
+    def red(out, in_): do("v", lambda q: q.tensor_reduce(out=A(out), in_=A(in_), axis=AxisListType.X, op=OP.add), [in_], [out])
+
+    def act(out, in_, **kw):
+        rd = [in_] + [s for s in kw.values() if isc(s)]
+        k2 = {k: (A(s) if isc(s) else s) for k, s in kw.items()}
+        do("s", lambda q: q.activation(out=A(out), in_=A(in_), func=COPY, **k2), rd, [out])
+
+    def mm(out, lhs, rhs, start=True, stop=True):
+        do("t", lambda q: q.matmul(out=A(out), lhsT=A(lhs), rhs=A(rhs), start=start, stop=stop), [lhs, rhs], [out], acc=not start)
+
+    def gather(e, out, win, lst):
+        if e == "v": do("v", lambda q: q.tensor_copy(out=A(out), in_=A(win).indirect(A(lst))), [win, lst], [out])
+        else: do("s", lambda q: q.activation(out=A(out), in_=A(win).indirect(A(lst)), func=COPY), [win, lst], [out])
+
+    def scatter(win, lst, in_): do("v", lambda q: q.tensor_copy(out=A(win).indirect(A(lst)), in_=A(in_)), [in_, lst], [win])
+
+    def iota(out, pattern, base, cm, imp=True):
+        if imp: do("g", lambda q: q.iota(A(out), pattern, base, cm, allow_small_or_imprecise_dtypes=True), [], [out])
+        else: do("g", lambda q: q.iota(A(out), pattern, base, cm), [], [out])
+
+    def c1(k): return ("col", k, k + 1)
+    PM, PG, PP, ZERO, KK, A16, NA0, IA0, INI, WGT, HIC, UW, P64 = 0, 1, 2, 3, 4, 8, 9, 10, 11, 12, 13, 14, 15
+
+    def w8(lo, hi, st=1): return T.v0[0:8, lo:hi] if st == 1 else T.v0[0:8, lo:hi:st]
+    dma("y", w8(0, 4096), T.w0[:, :], [], [("v0", 0, 4096)])
+    dma("s", T.zs[:], T.z0[:, :], [], [("zs", 0, 512)])
+    dma("y", T.ptb[:], T.pt[:, :], [], [("ptb", 0, 4096)])
+    dma("y", T.lmb[:], T.lm[:, :], [], [("lmb", 0, 1024)])
+
+    iota(("pidx", 0, 1), [[0, 1]], 0, 1, False)
+    iota(("xg", 0, 128), [[1, 8], [0, 16]], 0, 0)
+    iota(("xa", 0, 256), [[0, 16], [1, 16]], 0, 0)
+    fill(("v1", 0, 2048), 0.0)
+    cp(c1(PP), ("pidx", 0, 1))
+    ts(("b8", 0, 128), ("xg", 0, 128), c1(PP), OP.is_equal)
+    ts(("pidx", 1, 2), ("pidx", 0, 1), 15, OP.bitwise_and)
+    ts(("pidx", 2, 3), ("pidx", 0, 1), 4, OP.arith_shift_right)
+    for a in range(16):
+        o, i = ("v1", a * 128 + a, (a + 1) * 128, 16), ("b8", a, 128, 16)
+        do("s", lambda q: q.activation(out=T.v1[0:8, o[1]:o[2]:16], in_=T.b8[0:8, a:128:16], func=COPY), [i], [o])
+    iota(("big", 0, 2048), [[-100, 16], [1, 8], [100, 16]], 0, 0)
+    send(rank - 1, "zs", 0, 256, "zz0", 0, "a01")
+    send(rank - 2, "zs", 256, 384, "zz1", 128, "a2")
+    send(rank - 3, "zs", 384, 512, "zz2", 128, "a3")
+    arrives(rank + 1, "zz0", 0, 256, "a01")
+    arrives(rank + 2, "zz1", 128, 256, "a2")
+    arrives(rank + 3, "zz2", 128, 256, "a3")
+    iota(("i61", 0, 512), [[976, 128], [0, 4]], 0, 0)
+    iota(("q", 0, 256), [[0, 2], [1, 16], [0, 8]], 0, 0)
+    iota(("clf", 0, 16), [[512, 2], [0, 8]], 63, 0)
+    iota(("wm", 0, 8192), [[0, 8192]], 0, 0)
+
+    cp(c1(PM), ("pidx", 1, 2))
+    cp(c1(PG), ("pidx", 2, 3))
+    ts(("bd", 0, 128), ("xg", 0, 128), c1(PG), OP.is_equal)
+    ts(("ul", 0, 128), ("xa", 0, 128), c1(PM), OP.is_gt)
+    tt(("sl", 0, 128), ("bd", 0, 128), ("ul", 0, 128), OP.mult)
+    ts(c1(UW), c1(PM), 2.0, OP.mult, 1.0, OP.add)
+    ts(("ul", 0, 128), ("bd", 0, 128), c1(UW), OP.mult)
+    fill(("zer", 0, 256), 0.0)
+    ts(("dmk", 0, 256), ("xa", 0, 256), c1(PM), OP.is_equal)
+    ts(c1(IA0), c1(PM), 0.0, OP.is_equal)
+    ts(c1(NA0), c1(PM), 0.0, OP.is_gt)
+    ts(c1(INI), c1(IA0), -2.0, OP.mult, 1.0, OP.add)
+    ts(c1(WGT), c1(IA0), 17.0, OP.mult, -1.0, OP.add)
+    ts(c1(HIC), c1(IA0), 255.0, OP.mult, 1.0, OP.add)
+    ts(c1(ZERO), c1(NA0), -1.0, OP.mult)
+    for kk in range(4):
+        ts(c1(KK + kk), c1(PM), 4.0, OP.mult, float(3 + 64 * kk), OP.add)
+    fill(c1(A16), 0.0)
+    fill(("seg", 0, 256), 0.0)
+    fill(("seg", 0, 256, 16), -65536.0)
+    fill(("inc", 0, 1), 0.0)
+    fill(("hsb", 0, 1), 0.0)
+    fill(("we", 0, 4096), 0.0)
+    fill(("dm1", 0, CH), 0.0)
+    ts(("dm1", 0, CH), ("dm1", 0, CH), c1(ZERO), OP.add)
+    ts(("lw", 0, 2048), ("big", 0, 2048), c1(PG), OP.is_equal, c1(WGT), OP.mult)
+    for a in range(16):
+        act(("rb", a * 128, (a + 1) * 128), ("bd", 0, 128), scale=("dmk", a, a + 1))
+
+    for a in range(16):
+        do("t", lambda q: q.matmul(out=T.pe0[:, 0:256], lhsT=T.v1[0:8, a * 128:(a + 1) * 128], rhs=w8(a, 4096, 16), start=(a == 0),
+                                   stop=(a == 15)), [("v1", a * 128, (a + 1) * 128), ("v0", 0, 4096)], [("pe0", 0, 256)], acc=a > 0)
+    cp(("wl", 0, 256), ("pe0", 0, 256))
+
+    cnt = ["cnt0", "cnt1"]
+    pe = ["pe0", "pc"]
+    for t in range(3):
+        zz = "zz%d" % t
+        zn = "zn%d" % t
+        mm(("pcs", 0, 256), ("bd", 0, 128), ("wl", 0, 256))
+        mm(("pex", 0, 256), ("sl", 0, 128), ("wl", 0, 256))
+        if t == 0:
+            for b in range(8):
+                do("t", lambda q: q.matmul(out=T[cnt[b % 2]][:, 0:512], lhsT=T.b8[0:8, 0:128], rhs=w8(b * 512, (b + 1) * 512), start=True, stop=True),
+                   [("b8", 0, 128), ("v0", 0, 4096)], [(cnt[b % 2], 0, 512)])
+                act(("wr", b * 512, (b + 1) * 512), (cnt[b % 2], 0, 512))
+        else:
+            for b in range(8):
+                for a in (2 * b, 2 * b + 1):
+                    mm((cnt[b % 2], (a % 2) * 256, (a % 2) * 256 + 256), ("rb", a * 128, (a + 1) * 128), ("wl", 0, 256))
+                for a in (2 * b, 2 * b + 1):
+                    act(("wr", a, 4096, 16), (cnt[b % 2], (a % 2) * 256, (a % 2) * 256 + 256))
+        scan(("inc", 1, 257), ("pcs", 0, 256), ("zer", 0, 256), 0.0, OP.add, OP.add)
+        ts(("ti", 0, 1), ("inc", 256, 257), -0.5, OP.add, 0.5, OP.mult)
+        tt(("msk", 0, 256), ("inc", 0, 256), ("dmk", 0, 256), OP.mult)
+        ts(("tc", 0, 1), ("ti", 0, 1), 4096.0, OP.min, 1.0 / 2048, OP.mult)
+        tt(("db", 0, 256), ("inc", 0, 256), ("pex", 0, 256), OP.add)
+        do("v", lambda q: q.reciprocal(out=T.tc[:, 1:2], in_=T.tc[:, 0:1]), [("tc", 0, 1)], [("tc", 1, 2)])
+        scan(("sg", 0, 256), ("seg", 0, 256), ("msk", 0, 256), 0.0, OP.add, OP.max)
+        cp(("db", 256, 272), ("sg", 15, 256, 16))
+        ts(("ci", 0, 272), ("db", 0, 272), ("tc", 1, 2), OP.mult)
+        ts(("p1", 0, 272), ("ci", 0, 272), ("tc", 0, 1), OP.mult)
+        tt(("p1", 0, 272), ("p1", 0, 272), ("db", 0, 272), OP.is_lt)
+        tt(("hsb", 1, 273), ("ci", 0, 272), ("p1", 0, 272), OP.add)
+        cp(("offs", 0, 16), ("hsb", 257, 273))
+        tt(("dl", 0, 256), ("hsb", 1, 257), ("hsb", 0, 256), OP.subtract)
+        ts(("dlb", 0, 256), ("dl", 0, 256), c1(NA0), OP.mult, c1(IA0), OP.add)
+        scatter(("we", 0, 16384), ("offs", 0, 16), ("dlb", 0, 256))
+        mm(("pu", 0, 128), ("ul", 0, 128), (zz, 0, 128))
+        for hf in (0, 1):
+            lo, hi = hf * 2048, hf * 2048 + 2048
+            scan(("gg", lo, hi), ("we", lo, hi), ("dm1", 0, CH), c1(INI) if hf == 0 else ("gg", 2047, 2048), OP.add, OP.add)
+            ts(("v1", 4096 + lo, 4096 + hi), ("gg", lo, hi), 0.0, OP.max, c1(HIC), OP.min)
+            for a in range(16):
+                mm((pe[hf], 0, 128), ("lw", a * 128, (a + 1) * 128), ("v1", 4096 + lo + a, 4096 + hi, 16), a == 0, a == 15)
+        if t < 2: iota(("we", 0, 4096), [[0, 4096]], 0, 0)
+        ts(("el", 0, 128), (pe[0], 0, 128), 15.0, OP.add)
+        gather("s", ("ph", 0, 2048), ("ptb", 0, 4096), ("el", 0, 128))
+        for kk in range(4):
+            ts(("pt1", kk, 512, 4), ("pu", 0, 128), c1(KK + kk), OP.mult, c1(A16), OP.add)
+        ts(("el", 128, 256), (pe[1], 0, 128), 15.0, OP.add)
+        gather("s", ("ph", 2048, 2816), ("ptb", 0, 4096), ("el", 128, 176))
+        tt(("hi", 0, 512), ("pt1", 0, 512), ("i61", 0, 512), OP.add)
+        ts(("hi", 0, 512), ("hi", 0, 512), 4, OP.arith_shift_right, 4095, OP.bitwise_and)
+        cp(("hl", 0, 512), ("hi", 0, 512))
+        gather("v", ("ph", 2816, 4096), ("ptb", 0, 4096), ("el", 176, 256))
+        gather("s", ("net", 16, 16 + 1024), ("ph", 0, 4096), ("hl", 0, 64))
+        gather("v", ("net", 16 + 1024, AW), ("ph", 0, 4096), ("hl", 64, 128))
+        for c in range(1, 4):
+            gather("s", ("net", c * AW + 16, (c + 1) * AW), ("ph", 0, 4096), ("hl", c * 128, (c + 1) * 128))
+        if t == 0:
+            for c in range(4): fill(("net", c * AW, c * AW + 16), 0.0)
+            ts(("cb", 0, 2048), ("big", 0, 2048), c1(PG), OP.is_equal)
+        for mr in (0, 1):
+            o = mr * 128
+            tt(("dz", o + 1, o + 128), (zz, o + 1, o + 128), (zz, o, o + 127), OP.subtract)
+            cp(("dz", o, o + 128, 32), (zz, o, o + 128, 32))
+        for c in range(4):
+            b0 = c * AW
+            vs = [("v0", c * CH, (c + 1) * CH), ("v1", c * CH, (c + 1) * CH)]
+            cp(("sh", 0, CH), ("net", b0 + 15, b0 + 15 + CH))
+            for mr in (0, 1):
+                tt(("sh", 0, CH, 64), ("net", b0 + 15, b0 + 15 + CH, 64), ("dz", mr * 128 + c * 32, mr * 128 + c * 32 + 32), OP.add)
+                scan(vs[mr], ("net", b0 + 16, b0 + AW), ("sh", 0, CH), -OFF, OP.add, OP.subtract)
+                ts(vs[mr], vs[mr], -OFF, OP.is_equal)
+                for s in range(4):
+                    k = 4 * c + s
+                    mm((cnt[mr], 0, 512), ("cb", k * 128, (k + 1) * 128), ("v%d" % mr, c * CH + s * 512, c * CH + (s + 1) * 512), k == 0, k == 15)
+        if t == 0:
+            for msk, val in (("mxm", -512.0), ("mnm", 512.0)):
+                fill((msk, 0, CH), 0.0)
+                fill((msk, 0, CH, 64), val)
+            ts(("mc", 0, 256), ("q", 0, 256), c1(PM), OP.is_equal)
+            ts(("pidx", 3, 4), ("pidx", 0, 1), 7, OP.bitwise_and)
+            ts(c1(P64), ("pidx", 3, 4), 64.0, OP.mult)
+            ts(("cl", 0, 16), ("clf", 0, 16), c1(P64), OP.add)
+        for b in (0, 1):
+            o = b * 128
+            cp(("lf", o, o + 128), ("lmb", t * 256 + b, (t + 1) * 256, 2))
+            tt(("ldiff", o, o + 128), ("lmb", (t + 1) * 256 + b, (t + 2) * 256, 2), ("lf", o, o + 128), OP.subtract)
+        for mr in (0, 1):
+            scan(("cm", mr * 512, mr * 512 + 512), ("mxm", 0, 512), (cnt[mr], 0, 512), 0.0, OP.add, OP.max)
+        do("v", lambda q: q.tensor_tensor(out=T.cx[:, 0:256], in0=T.cm[:, 0:1024].indirect(T.cl[:, 0:16]), in1=T.mc[:, 0:256], op=OP.mult),
+           [("cm", 0, 1024), ("cl", 0, 16), ("mc", 0, 256)], [("cx", 0, 256)])
+        for k in range(3):
+            o = 0 if k < 2 else 128
+            mm(("pc", k * 128, k * 128 + 128), ("bd", 0, 128), ("cx", o, o + 128))
+        ts(("m", 0, 256), ("pc", 0, 256), 12.0, OP.is_ge)
+        tt(("t0", 0, 256), ("m", 0, 256), ("ldiff", 0, 256), OP.mult)
+        tt(("slf", 0, 256), ("t0", 0, 256), ("lf", 0, 256), OP.add)
+        cp(("so", 0, 256), ("slf", 0, 256))
+        for b in (0, 1):
+            gather("s", ("gg", b * 2048, b * 2048 + 2048), ("wr", 0, 4096), ("so", b * 128, b * 128 + 128))
+        ts(("h1", 0, 128), ("pc", 256, 384), 12.0, OP.is_ge)
+        ts(("bm", 0, 256), ("m", 0, 256), 4096.0, OP.mult, 8192.0, OP.add)
+        tt(("hh", 0, 128), ("h1", 0, 128), ("m", 0, 128), OP.mult)
+        tt(("bm", 0, 256), ("bm", 0, 256), ("slf", 0, 256), OP.add)
+        ts(("pen", 0, 128), ("hh", 0, 128), 256.0, OP.mult)
+        ts(("selz", 0, 128), ("m", 0, 128), -1.0, OP.mult, 1.0, OP.add)
+        tt(("selz", 128, 256), ("m", 0, 128), ("hh", 0, 128), OP.subtract)
+        red(("tc", 2, 3), ("hh", 0, 128))
+        mm(("pt1", 0, 128), ("bd", 0, 128), ("pen", 0, 128), True, False)
+        for b in range(32):
+            o = (b // 16) * 2048
+            mm(("pt1", 0, 128), ("bd", 0, 128), ("gg", o + b % 16, o + 2048, 16), False, b == 31)
+        for c in range(4):
+            src = ("net", c * AW + 16, (c + 1) * AW)
+            scan(("v0", c * CH, (c + 1) * CH), ("mxm", 0, CH), src, 0.0, OP.add, OP.max)
+            scan(("v1", c * CH, (c + 1) * CH), ("mnm", 0, CH), src, 0.0, OP.add, OP.min)
+
+        def centres():
+            tt(("ys", 0, 128), ("v0", 63, 8192, 64), ("v1", 63, 8192, 64), OP.add)
+            for o in (0, 128):
+                ts(("y2", o, o + 128), ("ys", 0, 128), 0.5, OP.mult, -0.25, OP.add)
+            tt(("q", 0, 256), ("y2", 0, 256), (zz, 0, 256), OP.add)
+            ts(("qi", 0, 256), ("q", 0, 256), 0.5, OP.mult, -0.25, OP.add)
+            tt(("q", 0, 256), ("qi", 0, 256), (zz, 0, 256), OP.subtract)
+            tt(("q", 0, 256), ("q", 0, 256), ("selz", 0, 256), OP.mult)
+            tt((zn, 0, 256), ("q", 0, 256), (zz, 0, 256), OP.add)
+            owner = rank + 1 + t
+            if t < 2:
+                send(rank - 1, zn, 128, 256, "zz%d" % (t + 1), 0, "ac%d" % (t + 1))
+                send(owner, zn, 0, 128, "zf", t * 128, "af%d" % t)
+                arrives(rank + 1, "zz%d" % (t + 1), 0, 128, "ac%d" % (t + 1))
+                arrives(rank - 1 - t, "zf", t * 128, t * 128 + 128, "af%d" % t)
+            else:
+                send(owner, zn, 0, 256, "zf", 256, "af2")
+                arrives(rank - 1 - t, "zf", 256, 512, "af2")
+
+        if t == 2: centres()
+        ts(("mk8", 0, 128), ("pt1", 0, 128), 768.0, OP.is_lt, -8192.0, OP.mult)
+        for o in (0, 128):
+            tt(("bm", o, o + 128), ("bm", o, o + 128), ("mk8", 0, 128), OP.add)
+        cp(("mo", 0, 256), ("bm", 0, 256))
+        scatter(("wm", 0, 16384), ("mo", 0, 256), ("gg", 0, 4096))
+        n = 0
+        for reg in (0, 4096):
+            for a in range(16):
+                mm(("pe0", 0, 256), ("cb", a * 128, (a + 1) * 128), ("wm", reg + a, reg + 4096, 16), n == 0, n == 31)
+                n += 1
+        if t < 2: centres()
+        red(("tc", 3, 4), ("mk8", 0, 128))
+        ts(("tc", 4, 5), ("tc", 3, 4), 1.0 / 8192, OP.mult, 128.0, OP.add)
+        tt(("ab", t, t + 1), ("tc", 4, 5), ("tc", 2, 3), OP.subtract)
+        if t < 2:
+            ts(c1(A16), ("ab", t, t + 1), 16.0, OP.mult)
+            iota(("wm", 0, 8192), [[0, 8192]], 0, 0)
+        ts(("t0", 0, 256), ("pe0", 0, 256), 1.0, OP.min, 1.0, OP.add)
+        tt(("t0", 0, 256), ("t0", 0, 256), ("wl", 0, 256), OP.mult)
+        ts(("w1", 0, 256), ("t0", 0, 256), 8.0, OP.min)
+        mm(("pcs", 0, 256), ("bd", 0, 128), ("w1", 0, 256))
+        red(("tc", 5, 6), ("pcs", 0, 256))
+        ts(("tc", 6, 7), ("tc", 5, 6), 7168.0, OP.is_le, 0.5, OP.max)
+        ts(("tc", 7, 8), ("tc", 5, 6), 7168.0, OP.is_gt, 0.25, OP.mult)
+        ts(("wi", 0, 256), ("w1", 0, 256), ("tc", 6, 7), OP.mult, ("tc", 7, 8), OP.add)
+        cp(("wl", 0, 256), ("wi", 0, 256))
+
+    dma("y", T.ya[:, :], T.ab[0:128:16, 0:3], [("ab", 0, 3)], [])
+    dma("s", T.yz[:, 0:256], T.zf[:, 0:256], [("zf", 0, 256)], [])
+    for a in range(16):
+        pb = ["cnt0", "cnt1", "pex", "pu"][a % 4]
+        mm((pb, 0, 256), ("rb", a * 128, (a + 1) * 128), ("wl", 0, 256))
+        if a % 2: act(("big", a, 4096, 16), (pb, 0, 256))
+        else: cp(("big", a, 4096, 16), (pb, 0, 256))
+    dma("y", T.yw[:, :], T.big[0:128:16, 0:4096], [("big", 0, 4096)], [])
+    dma("s", T.yz[:, 256:512], T.zf[:, 256:512], [("zf", 256, 512)], [])
+    for s, v in total.items():
+        if known["g"].get(s, 0) < v: g.wait_ge(T.sem[s], v)

@@ -2,25 +2,29 @@ from concourse.mybir import AluOpType, AxisListType, ActivationFunctionType
 
 OP = AluOpType
 COPY = ActivationFunctionType.Copy
+IDENT = ActivationFunctionType.Identity
+SILU = ActivationFunctionType.Silu
 OFF = 24576.0
 CH = 2048
 AW = CH + 16
+WE = 4368
 PSUM = ["pcs", "pex", "pu", "pt1", "pe0", "cnt0", "cnt1", "pc"]
 F, H, I32, U16, H16 = "float32", "bfloat16", "int32", "uint16", "float16"
 _SB = {
     "ptb": (4096, H), "lmb": (1024, I32), "lf": (256, F), "ldiff": (256, F), "ph": (4096, H), "net": (4 * AW, H),
-    "sh": (CH, H16), "v0": (8192, H), "v1": (8192, H), "wr": (4096, H), "gg": (4096, H),
-    "wm": (16384, H), "we": (16384, H), "big": (4096, F),
-    "cb": (2048, H), "lw": (2048, H), "rb": (2048, H), "mxm": (CH, H), "mnm": (CH, H), "dm1": (CH, H),
-    "pidx": (4, I32), "col": (32, F), "xa": (256, F), "xg": (128, F), "dmk": (256, F), "bd": (128, H),
-    "sl": (128, H), "ul": (128, H), "b8": (128, H), "mc": (256, H), "clf": (16, F), "cl": (16, U16),
+    "sh0": (CH, H16), "sh1": (CH, H16), "v0": (8192, H), "v1": (8192, H), "wr": (4096, H), "gg": (4096, H),
+    "wm": (16384, H), "we": (WE, H), "big": (4096, F), "dat": (4096, F), "lu": (768, U16), "rl": (768, U16),
+    "cb": (2048, H), "lw": (2048, H), "rb": (2048, H), "mxm": (CH, H), "mnm": (CH, H), "dm1": (CH, H), "xm": (CH, H),
+    "pidx": (4, I32), "col": (32, F), "xa": (256, F), "xg": (128, F), "dmk": (256, F), "bd": (128, H), "idn": (128, H),
+    "sl": (128, H), "ul": (128, H), "b8": (128, H), "mc": (256, H), "clf": (16, F), "cl": (16, U16), "cap": (16, F),
     "i61": (512, F), "zer": (256, F), "seg": (256, H), "zs": (512, H), "zz0": (256, H), "zz1": (256, H), "zz2": (256, H),
-    "zf": (512, H), "dz": (256, H), "wl": (256, H), "w1": (256, H), "wi": (256, I32), "inc": (264, F), "ti": (8, I32),
-    "tc": (8, F), "db": (272, F), "msk": (256, F), "sg": (256, F), "ci": (272, I32), "p1": (272, F),
-    "hsb": (280, F), "offs": (16, U16), "dl": (256, F), "dlb": (256, H), "el": (256, U16), "hi": (512, I32), "hl": (512, U16),
+    "zf": (512, H), "dz": (256, H), "nzt": (256, H), "wl": (256, H), "w1": (256, H), "wi": (256, I32), "inc": (264, F),
+    "ti": (8, I32), "tc": (8, F), "db": (272, F), "ci": (272, I32), "p1": (272, F),
+    "hsb": (280, F), "offs": (16, U16), "dlb": (256, H), "el": (256, U16), "hi": (512, I32), "hl": (512, U16),
     "cm": (1024, H), "cx": (256, H), "m": (256, F), "t0": (256, F), "slf": (256, F), "so": (256, U16), "bm": (256, F),
-    "h1": (128, F), "hh": (128, F), "pen": (128, H), "selz": (256, F), "mk8": (128, F), "mo": (256, U16), "ab": (8, F),
-    "ys": (128, F), "y2": (256, I32), "q": (256, F), "qi": (256, I32), "zn0": (256, H), "zn1": (256, H), "zn2": (256, H),
+    "h1": (128, F), "hh": (128, F), "pen": (128, H), "selz": (256, F), "mk8": (128, F), "mo": (256, U16), "mw": (256, H),
+    "ab": (8, F), "ys": (128, F), "y2": (256, I32), "q": (256, F), "qi": (256, I32), "zn0": (256, H), "zn1": (256, H),
+    "zn2": (256, H),
 }
 SCRATCH = {k: ("sbuf", [128, n], d) for k, (n, d) in _SB.items()}
 for _k in PSUM:
@@ -150,10 +154,10 @@ def rank_program(g, core, T, topo):
     def fill(out, c): do("v", lambda q: q.memset(A(out), c), [], [out])
     def red(out, in_): do("v", lambda q: q.tensor_reduce(out=A(out), in_=A(in_), axis=AxisListType.X, op=OP.add), [in_], [out])
 
-    def act(out, in_, **kw):
+    def act(out, in_, func=COPY, **kw):
         rd = [in_] + [s for s in kw.values() if isc(s)]
         k2 = {k: (A(s) if isc(s) else s) for k, s in kw.items()}
-        do("s", lambda q: q.activation(out=A(out), in_=A(in_), func=COPY, **k2), rd, [out])
+        do("s", lambda q: q.activation(out=A(out), in_=A(in_), func=func, **k2), rd, [out])
 
     def mm(out, lhs, rhs, start=True, stop=True):
         do("t", lambda q: q.matmul(out=A(out), lhsT=A(lhs), rhs=A(rhs), start=start, stop=stop), [lhs, rhs], [out], acc=not start)
@@ -171,6 +175,19 @@ def rank_program(g, core, T, topo):
     def c1(k): return ("col", k, k + 1)
     PM, PG, PP, ZERO, KK, A16, NA0, IA0, INI, WGT, HIC, UW, P64 = 0, 1, 2, 3, 4, 8, 9, 10, 11, 12, 13, 14, 15
 
+    def inverse(c, half):
+        o = (c - 1) * 256 + half * 128
+        win, lst, src = ("big", 0, 4096), ("lu", o, o + 128), ("dat", half * 2048, half * 2048 + 2048)
+        do("s", lambda q: q.activation(out=A(win).indirect(A(lst)), in_=A(src), func=SILU), [lst, src], [win])
+
+    def inverse_rows(buf, lo): act((buf, lo, lo + 4096), ("big", 0, 4096))
+
+    def inverse_list(bank, buf, lo):
+        for a in range(16):
+            mm((bank, 0, 256), ("cb", a * 128, (a + 1) * 128), (buf, lo + a, lo + 4096, 16), a == 0, a == 15)
+
+    def inverse_done(c, bank): ts(("rl", (c - 1) * 256, c * 256), (bank, 0, 256), 0.0625, OP.mult, -32.0, OP.add)
+
     def w8(lo, hi, st=1): return T.v0[0:8, lo:hi] if st == 1 else T.v0[0:8, lo:hi:st]
     dma("y", w8(0, 4096), T.w0[:, :], [], [("v0", 0, 4096)])
     dma("s", T.zs[:], T.z0[:, :], [], [("zs", 0, 512)])
@@ -180,15 +197,30 @@ def rank_program(g, core, T, topo):
     iota(("pidx", 0, 1), [[0, 1]], 0, 1, False)
     iota(("xg", 0, 128), [[1, 8], [0, 16]], 0, 0)
     iota(("xa", 0, 256), [[0, 16], [1, 16]], 0, 0)
+    iota(("cap", 0, 16), [[16, 16]], 4096, 0)
     fill(("v1", 0, 2048), 0.0)
     cp(c1(PP), ("pidx", 0, 1))
-    ts(("b8", 0, 128), ("xg", 0, 128), c1(PP), OP.is_equal)
     ts(("pidx", 1, 2), ("pidx", 0, 1), 15, OP.bitwise_and)
+    ts(("b8", 0, 128), ("xg", 0, 128), c1(PP), OP.is_equal)
     ts(("pidx", 2, 3), ("pidx", 0, 1), 4, OP.arith_shift_right)
+    cp(c1(PM), ("pidx", 1, 2))
+    cp(c1(PG), ("pidx", 2, 3))
+    ts(c1(IA0), c1(PM), 0.0, OP.is_equal)
+    ts(("bd", 0, 128), ("xg", 0, 128), c1(PG), OP.is_equal)
+    ts(c1(NA0), c1(PM), 0.0, OP.is_gt)
+    ts(c1(WGT), c1(IA0), 17.0, OP.mult, -1.0, OP.add)
+    ts(c1(ZERO), c1(NA0), -1.0, OP.mult)
+    fill(("lw", 0, 2048), 0.0)
+    fill(("cb", 0, 2048), 0.0)
     for a in range(16):
         o, i = ("v1", a * 128 + a, (a + 1) * 128, 16), ("b8", a, 128, 16)
         do("s", lambda q: q.activation(out=T.v1[0:8, o[1]:o[2]:16], in_=T.b8[0:8, a:128:16], func=COPY), [i], [o])
-    iota(("big", 0, 2048), [[-100, 16], [1, 8], [100, 16]], 0, 0)
+    act(("dm1", 0, CH), ("cb", 0, CH), IDENT, bias=c1(ZERO))
+    for a in range(16):
+        act(("lw", a * 128 + a, (a + 1) * 128, 16), ("bd", a, 128, 16), scale=c1(WGT))
+    for o in (0, CH): act(("we", o, o + CH), ("cb", 0, CH))
+    for a in range(16):
+        act(("cb", a * 128 + a, (a + 1) * 128, 16), ("bd", a, 128, 16))
     send(rank - 1, "zs", 0, 256, "zz0", 0, "a01")
     send(rank - 2, "zs", 256, 384, "zz1", 128, "a2")
     send(rank - 3, "zs", 384, 512, "zz2", 128, "a3")
@@ -196,38 +228,34 @@ def rank_program(g, core, T, topo):
     arrives(rank + 2, "zz1", 128, 256, "a2")
     arrives(rank + 3, "zz2", 128, 256, "a3")
     iota(("i61", 0, 512), [[976, 128], [0, 4]], 0, 0)
+    iota(("xm", 0, CH), [[0, CH]], 1, 0)
+    do("g", lambda q: q.affine_select(A(("xm", 0, CH)), A(("xm", 0, CH)), [[-1, 32], [0, 64]], OP.is_equal, 0.0, -96, 1),
+       [("xm", 0, CH)], [("xm", 0, CH)])
+    iota(("mxm", 0, CH), [[0, CH]], 0, 0)
+    iota(("mnm", 0, CH), [[0, CH]], 0, 0)
+    iota(("dat", 0, 4096), [[1, 128], [0, 32]], 32, 0)
     iota(("q", 0, 256), [[0, 2], [1, 16], [0, 8]], 0, 0)
     iota(("clf", 0, 16), [[512, 2], [0, 8]], 63, 0)
     iota(("wm", 0, 8192), [[0, 8192]], 0, 0)
 
-    cp(c1(PM), ("pidx", 1, 2))
-    cp(c1(PG), ("pidx", 2, 3))
-    ts(("bd", 0, 128), ("xg", 0, 128), c1(PG), OP.is_equal)
     ts(("ul", 0, 128), ("xa", 0, 128), c1(PM), OP.is_gt)
+    ts(("dmk", 0, 256), ("xa", 0, 256), c1(PM), OP.is_equal)
     tt(("sl", 0, 128), ("bd", 0, 128), ("ul", 0, 128), OP.mult)
     ts(c1(UW), c1(PM), 2.0, OP.mult, 1.0, OP.add)
+    tt(("idn", 0, 128), ("bd", 0, 128), ("dmk", 0, 128), OP.mult)
     ts(("ul", 0, 128), ("bd", 0, 128), c1(UW), OP.mult)
     fill(("zer", 0, 256), 0.0)
-    ts(("dmk", 0, 256), ("xa", 0, 256), c1(PM), OP.is_equal)
-    ts(c1(IA0), c1(PM), 0.0, OP.is_equal)
-    ts(c1(NA0), c1(PM), 0.0, OP.is_gt)
     ts(c1(INI), c1(IA0), -2.0, OP.mult, 1.0, OP.add)
-    ts(c1(WGT), c1(IA0), 17.0, OP.mult, -1.0, OP.add)
     ts(c1(HIC), c1(IA0), 255.0, OP.mult, 1.0, OP.add)
-    ts(c1(ZERO), c1(NA0), -1.0, OP.mult)
     for kk in range(4):
         ts(c1(KK + kk), c1(PM), 4.0, OP.mult, float(3 + 64 * kk), OP.add)
+    ts(("cap", 0, 16), ("cap", 0, 16), c1(PM), OP.add)
     fill(c1(A16), 0.0)
     fill(("seg", 0, 256), 0.0)
-    fill(("seg", 0, 256, 16), -65536.0)
     fill(("inc", 0, 1), 0.0)
     fill(("hsb", 0, 1), 0.0)
-    fill(("we", 0, 4096), 0.0)
-    fill(("dm1", 0, CH), 0.0)
-    ts(("dm1", 0, CH), ("dm1", 0, CH), c1(ZERO), OP.add)
-    ts(("lw", 0, 2048), ("big", 0, 2048), c1(PG), OP.is_equal, c1(WGT), OP.mult)
-    for a in range(16):
-        act(("rb", a * 128, (a + 1) * 128), ("bd", 0, 128), scale=("dmk", a, a + 1))
+    fill(("seg", 0, 256, 16), -65536.0)
+    for c in range(4): fill(("net", c * AW, c * AW + 16), 0.0)
 
     for a in range(16):
         do("t", lambda q: q.matmul(out=T.pe0[:, 0:256], lhsT=T.v1[0:8, a * 128:(a + 1) * 128], rhs=w8(a, 4096, 16), start=(a == 0),
@@ -252,23 +280,27 @@ def rank_program(g, core, T, topo):
                     mm((cnt[b % 2], (a % 2) * 256, (a % 2) * 256 + 256), ("rb", a * 128, (a + 1) * 128), ("wl", 0, 256))
                 for a in (2 * b, 2 * b + 1):
                     act(("wr", a, 4096, 16), (cnt[b % 2], (a % 2) * 256, (a % 2) * 256 + 256))
+            inverse_rows("wm", 8192)
         scan(("inc", 1, 257), ("pcs", 0, 256), ("zer", 0, 256), 0.0, OP.add, OP.add)
         ts(("ti", 0, 1), ("inc", 256, 257), -0.5, OP.add, 0.5, OP.mult)
-        tt(("msk", 0, 256), ("inc", 0, 256), ("dmk", 0, 256), OP.mult)
+        tt(("t0", 0, 256), ("inc", 0, 256), ("dmk", 0, 256), OP.mult)
         ts(("tc", 0, 1), ("ti", 0, 1), 4096.0, OP.min, 1.0 / 2048, OP.mult)
-        tt(("db", 0, 256), ("inc", 0, 256), ("pex", 0, 256), OP.add)
+        scan(("slf", 0, 256), ("seg", 0, 256), ("t0", 0, 256), 0.0, OP.add, OP.max)
         do("v", lambda q: q.reciprocal(out=T.tc[:, 1:2], in_=T.tc[:, 0:1]), [("tc", 0, 1)], [("tc", 1, 2)])
-        scan(("sg", 0, 256), ("seg", 0, 256), ("msk", 0, 256), 0.0, OP.add, OP.max)
-        cp(("db", 256, 272), ("sg", 15, 256, 16))
+        tt(("db", 0, 256), ("inc", 0, 256), ("pex", 0, 256), OP.add)
+        cp(("db", 256, 272), ("slf", 15, 256, 16))
         ts(("ci", 0, 272), ("db", 0, 272), ("tc", 1, 2), OP.mult)
         ts(("p1", 0, 272), ("ci", 0, 272), ("tc", 0, 1), OP.mult)
         tt(("p1", 0, 272), ("p1", 0, 272), ("db", 0, 272), OP.is_lt)
         tt(("hsb", 1, 273), ("ci", 0, 272), ("p1", 0, 272), OP.add)
+        tt(("hsb", 257, 273), ("hsb", 257, 273), ("cap", 0, 16), OP.min)
+        tt(("bm", 0, 256), ("hsb", 1, 257), ("hsb", 0, 256), OP.subtract)
         cp(("offs", 0, 16), ("hsb", 257, 273))
-        tt(("dl", 0, 256), ("hsb", 1, 257), ("hsb", 0, 256), OP.subtract)
-        ts(("dlb", 0, 256), ("dl", 0, 256), c1(NA0), OP.mult, c1(IA0), OP.add)
-        scatter(("we", 0, 16384), ("offs", 0, 16), ("dlb", 0, 256))
+        ts(("dlb", 0, 256), ("bm", 0, 256), c1(NA0), OP.mult, c1(IA0), OP.add)
+        scatter(("we", 0, WE), ("offs", 0, 16), ("dlb", 0, 256))
         mm(("pu", 0, 128), ("ul", 0, 128), (zz, 0, 128))
+        for mr in (0, 1):
+            mm(("pu", 128 + mr * 128, 256 + mr * 128), (zz, mr * 128, mr * 128 + 128), ("idn", 0, 128))
         for hf in (0, 1):
             lo, hi = hf * 2048, hf * 2048 + 2048
             scan(("gg", lo, hi), ("we", lo, hi), ("dm1", 0, CH), c1(INI) if hf == 0 else ("gg", 2047, 2048), OP.add, OP.add)
@@ -280,46 +312,84 @@ def rank_program(g, core, T, topo):
         gather("s", ("ph", 0, 2048), ("ptb", 0, 4096), ("el", 0, 128))
         for kk in range(4):
             ts(("pt1", kk, 512, 4), ("pu", 0, 128), c1(KK + kk), OP.mult, c1(A16), OP.add)
-        ts(("el", 128, 256), (pe[1], 0, 128), 15.0, OP.add)
-        gather("s", ("ph", 2048, 2816), ("ptb", 0, 4096), ("el", 128, 176))
-        tt(("hi", 0, 512), ("pt1", 0, 512), ("i61", 0, 512), OP.add)
-        ts(("hi", 0, 512), ("hi", 0, 512), 4, OP.arith_shift_right, 4095, OP.bitwise_and)
-        cp(("hl", 0, 512), ("hi", 0, 512))
-        gather("v", ("ph", 2816, 4096), ("ptb", 0, 4096), ("el", 176, 256))
-        gather("s", ("net", 16, 16 + 1024), ("ph", 0, 4096), ("hl", 0, 64))
-        gather("v", ("net", 16 + 1024, AW), ("ph", 0, 4096), ("hl", 64, 128))
-        for c in range(1, 4):
-            gather("s", ("net", c * AW + 16, (c + 1) * AW), ("ph", 0, 4096), ("hl", c * 128, (c + 1) * 128))
-        if t == 0:
-            for c in range(4): fill(("net", c * AW, c * AW + 16), 0.0)
-            ts(("cb", 0, 2048), ("big", 0, 2048), c1(PG), OP.is_equal)
         for mr in (0, 1):
             o = mr * 128
             tt(("dz", o + 1, o + 128), (zz, o + 1, o + 128), (zz, o, o + 127), OP.subtract)
-            cp(("dz", o, o + 128, 32), (zz, o, o + 128, 32))
-        for c in range(4):
-            b0 = c * AW
-            vs = [("v0", c * CH, (c + 1) * CH), ("v1", c * CH, (c + 1) * CH)]
-            cp(("sh", 0, CH), ("net", b0 + 15, b0 + 15 + CH))
-            for mr in (0, 1):
-                tt(("sh", 0, CH, 64), ("net", b0 + 15, b0 + 15 + CH, 64), ("dz", mr * 128 + c * 32, mr * 128 + c * 32 + 32), OP.add)
-                scan(vs[mr], ("net", b0 + 16, b0 + AW), ("sh", 0, CH), -OFF, OP.add, OP.subtract)
-                ts(vs[mr], vs[mr], -OFF, OP.is_equal)
-                for s in range(4):
-                    k = 4 * c + s
-                    mm((cnt[mr], 0, 512), ("cb", k * 128, (k + 1) * 128), ("v%d" % mr, c * CH + s * 512, c * CH + (s + 1) * 512), k == 0, k == 15)
+        ts(("el", 128, 256), (pe[1], 0, 128), 15.0, OP.add)
+        gather("s", ("ph", 2048, 2816), ("ptb", 0, 4096), ("el", 128, 176))
+        tt(("hi", 0, 512), ("pt1", 0, 512), ("i61", 0, 512), OP.add)
+        cp(("dz", 0, 256, 32), (zz, 0, 256, 32))
+        ts(("hi", 0, 512), ("hi", 0, 512), 4, OP.arith_shift_right, 4095, OP.bitwise_and)
+        if t == 0: cp(("lu", 0, 768), ("lmb", 256, 1024))
+        cp(("hl", 0, 512), ("hi", 0, 512))
+        gather("v", ("ph", 2816, 4096), ("ptb", 0, 4096), ("el", 176, 256))
+        if t > 0: inverse_list("pt1", "wm", 8192)
+        gather("s", ("net", 16, 16 + 1024), ("ph", 0, 4096), ("hl", 0, 64))
+        gather("v", ("net", 16 + 1024, AW), ("ph", 0, 4096), ("hl", 64, 128))
+        for c in range(1, 4):
+            if c == 2: act(("nzt", 0, 256), ("pu", 128, 384), scale=-1.0)
+            gather("s", ("net", c * AW + 16, (c + 1) * AW), ("ph", 0, 4096), ("hl", c * 128, (c + 1) * 128))
+
+        def shift(c): cp(("sh%d" % (c % 2), 0, CH), ("net", c * AW + 15, c * AW + 15 + CH))
+
+        def begin(c, mr):
+            tt(("sh%d" % (c % 2), 0, CH, 64), ("net", c * AW + 15, c * AW + 15 + CH, 64), ("dz", mr * 128 + c * 32, mr * 128 + c * 32 + 32), OP.add)
+
+        def vv(c, mr): return ("v%d" % mr, c * CH, (c + 1) * CH)
+
+        def differ(c, mr): scan(vv(c, mr), ("net", c * AW + 16, (c + 1) * AW), ("sh%d" % (c % 2), 0, CH), -OFF, OP.add, OP.subtract)
+
+        def hits(c, mr):
+            ts(vv(c, mr), vv(c, mr), -OFF, OP.is_equal)
+            for s in range(4):
+                k = 4 * c + s
+                mm((cnt[mr], 0, 512), ("cb", k * 128, (k + 1) * 128), ("v%d" % mr, c * CH + s * 512, c * CH + (s + 1) * 512), k == 0, k == 15)
+
+        shift(0); begin(0, 0); differ(0, 0)
+        for c in range(3):
+            begin(c, 1)
+            if c < 2: shift(c + 1)
+            differ(c, 1)
+            if c < 2: begin(c + 1, 0)
+            hits(c, 0)
+            if c < 2: differ(c + 1, 0)
+            hits(c, 1)
+            if c == 0:
+                n = 0
+                for mr in (0, 1):
+                    for s in range(4):
+                        bank = "pcs" if n % 2 == 0 else "pex"
+                        n += 1
+                        mm((bank, 0, 512), ("idn", 0, 128), ("net", 3 * AW + 16 + s * 512, 3 * AW + 16 + (s + 1) * 512), True, False)
+                        mm((bank, 0, 512), ("nzt", mr * 128, mr * 128 + 128), ("xm", s * 512, (s + 1) * 512), False, True)
+                        act(("v%d" % mr, 3 * CH + s * 512, 3 * CH + (s + 1) * 512), (bank, 0, 512), bias=-OFF)
         if t == 0:
-            for msk, val in (("mxm", -512.0), ("mnm", 512.0)):
-                fill((msk, 0, CH), 0.0)
-                fill((msk, 0, CH, 64), val)
-            ts(("mc", 0, 256), ("q", 0, 256), c1(PM), OP.is_equal)
+            for a in range(16):
+                act(("rb", a * 128, (a + 1) * 128), ("bd", 0, 128), scale=("dmk", a, a + 1))
+        if t < 2: inverse(1 if t == 0 else 3, 0)
+        hits(3, 0)
+        hits(3, 1)
+        if t == 0:
+            fill(("mxm", 0, CH, 64), -512.0)
+            fill(("mnm", 0, CH, 64), 512.0)
             ts(("pidx", 3, 4), ("pidx", 0, 1), 7, OP.bitwise_and)
+            ts(("mc", 0, 256), ("q", 0, 256), c1(PM), OP.is_equal)
             ts(c1(P64), ("pidx", 3, 4), 64.0, OP.mult)
-            ts(("cl", 0, 16), ("clf", 0, 16), c1(P64), OP.add)
+        else: inverse_done(t + 1, "pt1")
         for b in (0, 1):
             o = b * 128
             cp(("lf", o, o + 128), ("lmb", t * 256 + b, (t + 1) * 256, 2))
+        if t == 0: ts(("cl", 0, 16), ("clf", 0, 16), c1(P64), OP.add)
+        for b in (0, 1):
+            o = b * 128
             tt(("ldiff", o, o + 128), ("lmb", (t + 1) * 256 + b, (t + 2) * 256, 2), ("lf", o, o + 128), OP.subtract)
+
+        def extreme(c, which):
+            src = ("net", c * AW + 16, (c + 1) * AW)
+            if which == 0: scan(vv(c, 0), ("mxm", 0, CH), src, 0.0, OP.add, OP.max)
+            else: scan(vv(c, 1), ("mnm", 0, CH), src, 0.0, OP.add, OP.min)
+
+        extreme(0, 0)
         for mr in (0, 1):
             scan(("cm", mr * 512, mr * 512 + 512), ("mxm", 0, 512), (cnt[mr], 0, 512), 0.0, OP.add, OP.max)
         do("v", lambda q: q.tensor_tensor(out=T.cx[:, 0:256], in0=T.cm[:, 0:1024].indirect(T.cl[:, 0:16]), in1=T.mc[:, 0:256], op=OP.mult),
@@ -333,22 +403,30 @@ def rank_program(g, core, T, topo):
         cp(("so", 0, 256), ("slf", 0, 256))
         for b in (0, 1):
             gather("s", ("gg", b * 2048, b * 2048 + 2048), ("wr", 0, 4096), ("so", b * 128, b * 128 + 128))
+        if t == 0:
+            inverse(1, 1)
+            inverse_rows("ph", 0)
+            inverse(2, 0)
+            inverse(2, 1)
         ts(("h1", 0, 128), ("pc", 256, 384), 12.0, OP.is_ge)
-        ts(("bm", 0, 256), ("m", 0, 256), 4096.0, OP.mult, 8192.0, OP.add)
+        if t == 0: ts(("bm", 0, 256), ("m", 0, 256), 4096.0, OP.mult, 8192.0, OP.add)
+        else: ts(("selz", 0, 128), ("m", 0, 128), -1.0, OP.mult, 1.0, OP.add)
         tt(("hh", 0, 128), ("h1", 0, 128), ("m", 0, 128), OP.mult)
-        tt(("bm", 0, 256), ("bm", 0, 256), ("slf", 0, 256), OP.add)
+        if t == 0:
+            ts(("selz", 0, 128), ("m", 0, 128), -1.0, OP.mult, 1.0, OP.add)
+            tt(("bm", 0, 256), ("bm", 0, 256), ("slf", 0, 256), OP.add)
         ts(("pen", 0, 128), ("hh", 0, 128), 256.0, OP.mult)
-        ts(("selz", 0, 128), ("m", 0, 128), -1.0, OP.mult, 1.0, OP.add)
         tt(("selz", 128, 256), ("m", 0, 128), ("hh", 0, 128), OP.subtract)
         red(("tc", 2, 3), ("hh", 0, 128))
         mm(("pt1", 0, 128), ("bd", 0, 128), ("pen", 0, 128), True, False)
         for b in range(32):
             o = (b // 16) * 2048
             mm(("pt1", 0, 128), ("bd", 0, 128), ("gg", o + b % 16, o + 2048, 16), False, b == 31)
-        for c in range(4):
-            src = ("net", c * AW + 16, (c + 1) * AW)
-            scan(("v0", c * CH, (c + 1) * CH), ("mxm", 0, CH), src, 0.0, OP.add, OP.max)
-            scan(("v1", c * CH, (c + 1) * CH), ("mnm", 0, CH), src, 0.0, OP.add, OP.min)
+        if t == 0: inverse_list("pex", "ph", 0)
+        extreme(0, 1)
+        for c in range(1, 4):
+            extreme(c, 0)
+            extreme(c, 1)
 
         def centres():
             tt(("ys", 0, 128), ("v0", 63, 8192, 64), ("v1", 63, 8192, 64), OP.add)
@@ -369,25 +447,48 @@ def rank_program(g, core, T, topo):
                 send(owner, zn, 0, 256, "zf", 256, "af2")
                 arrives(rank - 1 - t, "zf", 256, 512, "af2")
 
-        if t == 2: centres()
-        ts(("mk8", 0, 128), ("pt1", 0, 128), 768.0, OP.is_lt, -8192.0, OP.mult)
-        for o in (0, 128):
-            tt(("bm", o, o + 128), ("bm", o, o + 128), ("mk8", 0, 128), OP.add)
-        cp(("mo", 0, 256), ("bm", 0, 256))
-        scatter(("wm", 0, 16384), ("mo", 0, 256), ("gg", 0, 4096))
-        n = 0
-        for reg in (0, 4096):
-            for a in range(16):
-                mm(("pe0", 0, 256), ("cb", a * 128, (a + 1) * 128), ("wm", reg + a, reg + 4096, 16), n == 0, n == 31)
-                n += 1
+        if t == 0:
+            ts(("mk8", 0, 128), ("pt1", 0, 128), 768.0, OP.is_lt, -8192.0, OP.mult)
+            for o in (0, 128):
+                tt(("bm", o, o + 128), ("bm", o, o + 128), ("mk8", 0, 128), OP.add)
+            cp(("mo", 0, 256), ("bm", 0, 256))
+            scatter(("wm", 0, 16384), ("mo", 0, 256), ("gg", 0, 4096))
+            n = 0
+            for reg in (0, 4096):
+                for a in range(16):
+                    mm(("pe0", 0, 256), ("cb", a * 128, (a + 1) * 128), ("wm", reg + a, reg + 4096, 16), n == 0, n == 31)
+                    n += 1
+        else:
+            if t == 2: centres()
+            ts(("mk8", 0, 128), ("pt1", 0, 128), 768.0, OP.is_lt, -8192.0, OP.mult)
+            for o in (0, 128):
+                tt(("mw", o, o + 128), ("mk8", 0, 128), ("selz", o, o + 128), OP.mult)
+
+            def member(e, m, lo, hi):
+                r = (t - 1 + m) * 256
+                gather(e, ("wm", m * 4096 + lo, m * 4096 + hi), ("mw", m * 128, m * 128 + 128), ("rl", r + lo // 16, r + hi // 16))
+
+            for hf in (0, 1):
+                lo, hi = hf * 2048, hf * 2048 + 2048
+                cut = hi - 1024 if hf == 1 and t == 1 else hi
+                member("s", 0, lo, hi)
+                member("v", 1, lo, cut)
+                if cut < hi: member("s", 1, cut, hi)
+                n = 0
+                for reg in (0, 4096):
+                    for a in range(16):
+                        o = reg + lo
+                        mm(("pe0", hf * 128, hf * 128 + 128), ("cb", a * 128, (a + 1) * 128), ("wm", o + a, o + 2048, 16), n == 0, n == 31)
+                        n += 1
         if t < 2: centres()
+        if t == 0: inverse_done(1, "pex")
+        if t == 1: inverse(3, 1)
         red(("tc", 3, 4), ("mk8", 0, 128))
         ts(("tc", 4, 5), ("tc", 3, 4), 1.0 / 8192, OP.mult, 128.0, OP.add)
         tt(("ab", t, t + 1), ("tc", 4, 5), ("tc", 2, 3), OP.subtract)
-        if t < 2:
-            ts(c1(A16), ("ab", t, t + 1), 16.0, OP.mult)
-            iota(("wm", 0, 8192), [[0, 8192]], 0, 0)
-        ts(("t0", 0, 256), ("pe0", 0, 256), 1.0, OP.min, 1.0, OP.add)
+        if t < 2: ts(c1(A16), ("ab", t, t + 1), 16.0, OP.mult)
+        if t == 0: ts(("t0", 0, 256), ("pe0", 0, 256), 1.0, OP.min, 1.0, OP.add)
+        else: ts(("t0", 0, 256), ("pe0", 0, 256), 0.0, OP.is_lt, 1.0, OP.add)
         tt(("t0", 0, 256), ("t0", 0, 256), ("wl", 0, 256), OP.mult)
         ts(("w1", 0, 256), ("t0", 0, 256), 8.0, OP.min)
         mm(("pcs", 0, 256), ("bd", 0, 128), ("w1", 0, 256))

from concourse.mybir import AluOpType, AxisListType, ActivationFunctionType

OP = AluOpType
COPY = ActivationFunctionType.Copy
IDENT = ActivationFunctionType.Identity
SILU = ActivationFunctionType.Silu
OFF = 24576.0
CH = 2048
AW = CH + 16
WE = 4368
PSUM = ["pcs", "pex", "pu", "pt1", "pe0", "cnt0", "cnt1", "pc"]
F, H, I32, U16, H16 = "float32", "bfloat16", "int32", "uint16", "float16"
_SB = {
    "ptb": (4096, H), "lmb": (1024, I32), "lf": (256, F), "ldiff": (256, F), "ph": (4096, H), "net": (4 * AW, H),
    "sh0": (CH, H16), "sh1": (CH, H16), "v0": (8192, H), "v1": (8192, H), "wr": (4096, H), "gg": (4096, H),
    "wm": (16384, H), "we": (WE, H), "big": (4096, F), "dat": (4096, F), "lu": (768, U16), "rl": (768, U16),
    "cb": (2048, H), "lw": (2048, H), "rb": (2048, H), "mxm": (CH, H), "mnm": (CH, H), "dm1": (CH, H), "xm": (CH, H),
    "pidx": (4, I32), "col": (32, F), "xa": (256, F), "xg": (128, F), "dmk": (256, F), "bd": (128, H), "idn": (128, H),
    "sl": (128, H), "ul": (128, H), "b8": (128, H), "mc": (256, H), "clf": (16, F), "cl": (16, U16), "cap": (16, F),
    "i61": (512, F), "zer": (256, F), "seg": (256, H), "zs": (512, H), "zz0": (256, H), "zz1": (256, H), "zz2": (256, H),
    "zf": (512, H), "dz": (256, H), "nzt": (256, H), "wl": (256, H), "w1": (256, H), "wi": (256, I32), "inc": (264, F),
    "ti": (8, I32), "tc": (8, F), "db": (272, F), "ci": (272, I32), "p1": (272, F),
    "hsb": (280, F), "offs": (16, U16), "dlb": (256, H), "el": (256, U16), "hi": (512, I32), "hl": (512, U16),
    "cm": (1024, H), "cx": (256, H), "m": (256, F), "t0": (256, F), "slf": (256, F), "so": (256, U16), "bm": (256, F),
    "h1": (128, F), "hh": (128, F), "pen": (128, H), "selz": (256, F), "mk8": (128, F), "mo": (256, U16), "mw": (256, H),
    "ab": (8, F), "ys": (128, F), "y2": (256, I32), "q": (256, F), "qi": (256, I32), "zn0": (256, H), "zn1": (256, H),
    "zn2": (256, H),
}
SCRATCH = {k: ("sbuf", [128, n], d) for k, (n, d) in _SB.items()}
for _k in PSUM:
    SCRATCH[_k] = ("psum", [128, 512], "float32")
NDMA = 14
ARR = ["a01", "a2", "a3", "ac1", "ac2", "af0", "af1", "af2"]
SEMAPHORES = ["sv", "ss", "st", "sg"] + ["d%d" % k for k in range(NDMA)] + ["l%d" % k for k in range(8)] + ARR


def overlap(a, b):
    if a[0] >= b[1] or b[0] >= a[1]:
        return False
    if a[2] == b[2] and a[2] > 1 and (a[0] - b[0]) % a[2]:
        return False
    return True


def rank_program(g, core, T, topo):
    rank = T.rank_of(core)
    if rank is None:
        return
    N = len(T.cores)
    queues = {"v": g.vector, "s": g.scalar, "t": g.tensor, "g": g, "y": g.sync}
    csem = {"v": "sv", "s": "ss", "t": "st", "g": "sg"}
    known = {e: {} for e in queues}
    total = {}
    hist = {}
    ndma, nloc = [0], [0]

    def regs(items):
        out = []
        for it in items:
            if len(it) == 3: it = it + (1,)
            out.append(it)
        return out

    def order(e, reads, writes, acc):
        need = []
        for mode, items in (("r", reads), ("w", writes)):
            for (b, lo, hi, st) in items:
                for (pm, pe, reg, tok) in hist.get(b, []):
                    if b in PSUM and pe != e:
                        need.append(tok)
                        continue
                    if mode == "r" and pm == "r": continue
                    if acc and pe == e and mode == "w": continue
                    if overlap((lo, hi, st), reg): need.append(tok)
        todo = {}
        for (s, v, clk) in need:
            if known[e].get(s, 0) < v and (s not in todo or todo[s][0] < v):
                todo[s] = (v, clk)
        for s in sorted(todo, key=lambda x: -len(todo[x][1])):
            v, clk = todo[s]
            if known[e].get(s, 0) >= v: continue
            if any(o != s and known[e].get(o, 0) < todo[o][0] and todo[o][1].get(s, 0) >= v for o in todo): continue
            queues[e].wait_ge(T.sem[s], v)
            for k, x in clk.items():
                if known[e].get(k, 0) < x: known[e][k] = x
            known[e][s] = v

    def note(e, reads, writes, tok):
        for (b, lo, hi, st) in writes:
            keep = []
            for h in hist.get(b, []):
                r = h[2]
                if st == 1 and lo <= r[0] and r[1] <= hi and b not in PSUM: continue
                keep.append(h)
            hist[b] = keep + [("w", e, (lo, hi, st), tok)]
        for (b, lo, hi, st) in reads:
            hist.setdefault(b, []).append(("r", e, (lo, hi, st), tok))

    def do(e, fn, reads, writes, acc=False):
        reads, writes = regs(reads), regs(writes)
        order(e, reads, writes, acc)
        s = csem[e]
        total[s] = total.get(s, 0) + 1
        fn(queues[e]).then_inc(T.sem[s], 1)
        clk = dict(known[e]); clk[s] = total[s]
        note(e, reads, writes, (s, total[s], clk))

    def dma(e, out, in_, reads, writes):
        reads, writes = regs(reads), regs(writes)
        order(e, reads, writes, False)
        s = "d%d" % ndma[0]; ndma[0] += 1
        total[s] = 16
        queues[e].dma_start(out=out, in_=in_).then_inc(T.sem[s], 16)
        clk = dict(known[e]); clk[s] = 16
        note("dma" + s, reads, writes, (s, 16, clk))

    def send(dst_rank, buf, lo, hi, dbuf, dlo, rsem):
        dst = T.cores[dst_rank % N]
        order("g", [(buf, lo, hi, 1)], [], False)
        eng = topo.engines(core, dst)[:8:2]
        mask = sum(1 << x for x in eng)
        s = "l%d" % nloc[0]; nloc[0] += 1
        total[s] = len(eng)
        rid, pid, _se = topo.addr(dst)
        g.remote_dma(out_ap=T[dbuf][:, dlo:dlo + hi - lo], in_ap=T[buf][:, lo:hi], remote_sem=T.sem[rsem], local_sem=T.sem[s],
                     pid=pid, routing_id=rid, dma_engine_mask=mask)
        note("rem", [(buf, lo, hi, 1)], [], (s, len(eng), {s: len(eng)}))

    def arrives(src_rank, buf, lo, hi, rsem):
        n = len(topo.engines(T.cores[src_rank % N], core)[:8:2])
        total[rsem] = n
        note("arr", [], [(buf, lo, hi, 1)], (rsem, n, {rsem: n}))

    def A(x):
        return T[x[0]][:, x[1]:x[2]] if len(x) == 3 else T[x[0]][:, x[1]:x[2]:x[3]]

    def isc(x): return not isinstance(x, (int, float))

    def cp(out, in_): do("v", lambda q: q.tensor_copy(out=A(out), in_=A(in_)), [in_], [out])
    def tt(out, a, b, op): do("v", lambda q: q.tensor_tensor(out=A(out), in0=A(a), in1=A(b), op=op), [a, b], [out])

    def ts(out, a, s1, op0, s2=None, op1=None):
        rd = [a] + [s for s in (s1, s2) if s is not None and isc(s)]
        x1 = A(s1) if isc(s1) else s1
        x2 = A(s2) if s2 is not None and isc(s2) else s2
        if op1 is None: do("v", lambda q: q.tensor_scalar(out=A(out), in0=A(a), scalar1=x1, scalar2=None, op0=op0), rd, [out])
        else: do("v", lambda q: q.tensor_scalar(out=A(out), in0=A(a), scalar1=x1, scalar2=x2, op0=op0, op1=op1), rd, [out])

    def scan(out, d0, d1, init, op0, op1):
        rd = [d0, d1] + ([init] if isc(init) else [])
        x = A(init) if isc(init) else init
        do("v", lambda q: q.tensor_tensor_scan(A(out), A(d0), A(d1), x, op0, op1), rd, [out])

    def fill(out, c): do("v", lambda q: q.memset(A(out), c), [], [out])
    def red(out, in_): do("v", lambda q: q.tensor_reduce(out=A(out), in_=A(in_), axis=AxisListType.X, op=OP.add), [in_], [out])

    def act(out, in_, func=COPY, **kw):
        rd = [in_] + [s for s in kw.values() if isc(s)]
        k2 = {k: (A(s) if isc(s) else s) for k, s in kw.items()}
        do("s", lambda q: q.activation(out=A(out), in_=A(in_), func=func, **k2), rd, [out])

    def mm(out, lhs, rhs, start=True, stop=True):
        do("t", lambda q: q.matmul(out=A(out), lhsT=A(lhs), rhs=A(rhs), start=start, stop=stop), [lhs, rhs], [out], acc=not start)

    def gather(e, out, win, lst):
        if e == "v": do("v", lambda q: q.tensor_copy(out=A(out), in_=A(win).indirect(A(lst))), [win, lst], [out])
        else: do("s", lambda q: q.activation(out=A(out), in_=A(win).indirect(A(lst)), func=COPY), [win, lst], [out])

    def scatter(win, lst, in_): do("v", lambda q: q.tensor_copy(out=A(win).indirect(A(lst)), in_=A(in_)), [in_, lst], [win])

    def iota(out, pattern, base, cm, imp=True):
        if imp: do("g", lambda q: q.iota(A(out), pattern, base, cm, allow_small_or_imprecise_dtypes=True), [], [out])
        else: do("g", lambda q: q.iota(A(out), pattern, base, cm), [], [out])

    def c1(k): return ("col", k, k + 1)
    PM, PG, PP, ZERO, KK, A16, NA0, IA0, INI, WGT, HIC, UW, P64 = 0, 1, 2, 3, 4, 8, 9, 10, 11, 12, 13, 14, 15

    def inverse(c, half):
        o = (c - 1) * 256 + half * 128
        win, lst, src = ("big", 0, 4096), ("lu", o, o + 128), ("dat", half * 2048, half * 2048 + 2048)
        do("s", lambda q: q.activation(out=A(win).indirect(A(lst)), in_=A(src), func=SILU), [lst, src], [win])

    def inverse_rows(buf, lo): act((buf, lo, lo + 4096), ("big", 0, 4096))

    def inverse_list(bank, buf, lo):
        for a in range(16):
            mm((bank, 0, 256), ("cb", a * 128, (a + 1) * 128), (buf, lo + a, lo + 4096, 16), a == 0, a == 15)

    def inverse_done(c, bank): ts(("rl", (c - 1) * 256, c * 256), (bank, 0, 256), 0.0625, OP.mult, -32.0, OP.add)

    def w8(lo, hi, st=1): return T.v0[0:8, lo:hi] if st == 1 else T.v0[0:8, lo:hi:st]
    dma("y", w8(0, 4096), T.w0[:, :], [], [("v0", 0, 4096)])
    dma("s", T.zs[:], T.z0[:, :], [], [("zs", 0, 512)])
    dma("y", T.ptb[:], T.pt[:, :], [], [("ptb", 0, 4096)])
    dma("y", T.lmb[:], T.lm[:, :], [], [("lmb", 0, 1024)])

    iota(("pidx", 0, 1), [[0, 1]], 0, 1, False)
    iota(("xg", 0, 128), [[1, 8], [0, 16]], 0, 0)
    iota(("xa", 0, 256), [[0, 16], [1, 16]], 0, 0)
    iota(("cap", 0, 16), [[16, 16]], 4096, 0)
    fill(("v1", 0, 2048), 0.0)
    cp(c1(PP), ("pidx", 0, 1))
    ts(("pidx", 1, 2), ("pidx", 0, 1), 15, OP.bitwise_and)
    ts(("b8", 0, 128), ("xg", 0, 128), c1(PP), OP.is_equal)
    ts(("pidx", 2, 3), ("pidx", 0, 1), 4, OP.arith_shift_right)
    cp(c1(PM), ("pidx", 1, 2))
    cp(c1(PG), ("pidx", 2, 3))
    ts(c1(IA0), c1(PM), 0.0, OP.is_equal)
    ts(("bd", 0, 128), ("xg", 0, 128), c1(PG), OP.is_equal)
    ts(c1(NA0), c1(PM), 0.0, OP.is_gt)
    ts(c1(WGT), c1(IA0), 17.0, OP.mult, -1.0, OP.add)
    ts(c1(ZERO), c1(NA0), -1.0, OP.mult)
    fill(("lw", 0, 2048), 0.0)
    fill(("cb", 0, 2048), 0.0)
    for a in range(16):
        o, i = ("v1", a * 128 + a, (a + 1) * 128, 16), ("b8", a, 128, 16)
        do("s", lambda q: q.activation(out=T.v1[0:8, o[1]:o[2]:16], in_=T.b8[0:8, a:128:16], func=COPY), [i], [o])
    act(("dm1", 0, CH), ("cb", 0, CH), IDENT, bias=c1(ZERO))
    for a in range(16):
        act(("lw", a * 128 + a, (a + 1) * 128, 16), ("bd", a, 128, 16), scale=c1(WGT))
    for o in (0, CH): act(("we", o, o + CH), ("cb", 0, CH))
    for a in range(16):
        act(("cb", a * 128 + a, (a + 1) * 128, 16), ("bd", a, 128, 16))
    send(rank - 1, "zs", 0, 256, "zz0", 0, "a01")
    send(rank - 2, "zs", 256, 384, "zz1", 128, "a2")
    send(rank - 3, "zs", 384, 512, "zz2", 128, "a3")
    arrives(rank + 1, "zz0", 0, 256, "a01")
    arrives(rank + 2, "zz1", 128, 256, "a2")
    arrives(rank + 3, "zz2", 128, 256, "a3")
    iota(("i61", 0, 512), [[976, 128], [0, 4]], 0, 0)
    iota(("xm", 0, CH), [[0, CH]], 1, 0)
    do("g", lambda q: q.affine_select(A(("xm", 0, CH)), A(("xm", 0, CH)), [[-1, 32], [0, 64]], OP.is_equal, 0.0, -96, 1),
       [("xm", 0, CH)], [("xm", 0, CH)])
    iota(("mxm", 0, CH), [[0, CH]], 0, 0)
    iota(("mnm", 0, CH), [[0, CH]], 0, 0)
    iota(("dat", 0, 4096), [[1, 128], [0, 32]], 32, 0)
    iota(("q", 0, 256), [[0, 2], [1, 16], [0, 8]], 0, 0)
    iota(("clf", 0, 16), [[512, 2], [0, 8]], 63, 0)
    iota(("wm", 0, 8192), [[0, 8192]], 0, 0)

    ts(("ul", 0, 128), ("xa", 0, 128), c1(PM), OP.is_gt)
    ts(("dmk", 0, 256), ("xa", 0, 256), c1(PM), OP.is_equal)
    tt(("sl", 0, 128), ("bd", 0, 128), ("ul", 0, 128), OP.mult)
    ts(c1(UW), c1(PM), 2.0, OP.mult, 1.0, OP.add)
    tt(("idn", 0, 128), ("bd", 0, 128), ("dmk", 0, 128), OP.mult)
    ts(("ul", 0, 128), ("bd", 0, 128), c1(UW), OP.mult)
    fill(("zer", 0, 256), 0.0)
    ts(c1(INI), c1(IA0), -2.0, OP.mult, 1.0, OP.add)
    ts(c1(HIC), c1(IA0), 255.0, OP.mult, 1.0, OP.add)
    for kk in range(4):
        ts(c1(KK + kk), c1(PM), 4.0, OP.mult, float(3 + 64 * kk), OP.add)
    ts(("cap", 0, 16), ("cap", 0, 16), c1(PM), OP.add)
    fill(c1(A16), 0.0)
    fill(("seg", 0, 256), 0.0)
    fill(("inc", 0, 1), 0.0)
    fill(("hsb", 0, 1), 0.0)
    fill(("seg", 0, 256, 16), -65536.0)
    for c in range(4): fill(("net", c * AW, c * AW + 16), 0.0)

    for a in range(16):
        do("t", lambda q: q.matmul(out=T.pe0[:, 0:256], lhsT=T.v1[0:8, a * 128:(a + 1) * 128], rhs=w8(a, 4096, 16), start=(a == 0),
                                   stop=(a == 15)), [("v1", a * 128, (a + 1) * 128), ("v0", 0, 4096)], [("pe0", 0, 256)], acc=a > 0)
    cp(("wl", 0, 256), ("pe0", 0, 256))

    cnt = ["cnt0", "cnt1"]
    pe = ["pe0", "pc"]
    for t in range(3):
        zz = "zz%d" % t
        zn = "zn%d" % t
        mm(("pcs", 0, 256), ("bd", 0, 128), ("wl", 0, 256))
        mm(("pex", 0, 256), ("sl", 0, 128), ("wl", 0, 256))
        if t == 0:
            for b in range(8):
                do("t", lambda q: q.matmul(out=T[cnt[b % 2]][:, 0:512], lhsT=T.b8[0:8, 0:128], rhs=w8(b * 512, (b + 1) * 512), start=True, stop=True),
                   [("b8", 0, 128), ("v0", 0, 4096)], [(cnt[b % 2], 0, 512)])
                act(("wr", b * 512, (b + 1) * 512), (cnt[b % 2], 0, 512))
        else:
            for b in range(8):
                for a in (2 * b, 2 * b + 1):
                    mm((cnt[b % 2], (a % 2) * 256, (a % 2) * 256 + 256), ("rb", a * 128, (a + 1) * 128), ("wl", 0, 256))
                for a in (2 * b, 2 * b + 1):
                    act(("wr", a, 4096, 16), (cnt[b % 2], (a % 2) * 256, (a % 2) * 256 + 256))
            inverse_rows("wm", 8192)
        scan(("inc", 1, 257), ("pcs", 0, 256), ("zer", 0, 256), 0.0, OP.add, OP.add)
        ts(("ti", 0, 1), ("inc", 256, 257), -0.5, OP.add, 0.5, OP.mult)
        tt(("t0", 0, 256), ("inc", 0, 256), ("dmk", 0, 256), OP.mult)
        ts(("tc", 0, 1), ("ti", 0, 1), 4096.0, OP.min, 1.0 / 2048, OP.mult)
        scan(("slf", 0, 256), ("seg", 0, 256), ("t0", 0, 256), 0.0, OP.add, OP.max)
        do("v", lambda q: q.reciprocal(out=T.tc[:, 1:2], in_=T.tc[:, 0:1]), [("tc", 0, 1)], [("tc", 1, 2)])
        tt(("db", 0, 256), ("inc", 0, 256), ("pex", 0, 256), OP.add)
        cp(("db", 256, 272), ("slf", 15, 256, 16))
        ts(("ci", 0, 272), ("db", 0, 272), ("tc", 1, 2), OP.mult)
        ts(("p1", 0, 272), ("ci", 0, 272), ("tc", 0, 1), OP.mult)
        tt(("p1", 0, 272), ("p1", 0, 272), ("db", 0, 272), OP.is_lt)
        tt(("hsb", 1, 273), ("ci", 0, 272), ("p1", 0, 272), OP.add)
        tt(("hsb", 257, 273), ("hsb", 257, 273), ("cap", 0, 16), OP.min)
        tt(("bm", 0, 256), ("hsb", 1, 257), ("hsb", 0, 256), OP.subtract)
        cp(("offs", 0, 16), ("hsb", 257, 273))
        ts(("dlb", 0, 256), ("bm", 0, 256), c1(NA0), OP.mult, c1(IA0), OP.add)
        scatter(("we", 0, WE), ("offs", 0, 16), ("dlb", 0, 256))
        mm(("pu", 0, 128), ("ul", 0, 128), (zz, 0, 128))
        for mr in (0, 1):
            mm(("pu", 128 + mr * 128, 256 + mr * 128), (zz, mr * 128, mr * 128 + 128), ("idn", 0, 128))
        for hf in (0, 1):
            lo, hi = hf * 2048, hf * 2048 + 2048
            scan(("gg", lo, hi), ("we", lo, hi), ("dm1", 0, CH), c1(INI) if hf == 0 else ("gg", 2047, 2048), OP.add, OP.add)
            ts(("v1", 4096 + lo, 4096 + hi), ("gg", lo, hi), 0.0, OP.max, c1(HIC), OP.min)
            for a in range(16):
                mm((pe[hf], 0, 128), ("lw", a * 128, (a + 1) * 128), ("v1", 4096 + lo + a, 4096 + hi, 16), a == 0, a == 15)
        if t < 2: iota(("we", 0, 4096), [[0, 4096]], 0, 0)
        ts(("el", 0, 128), (pe[0], 0, 128), 15.0, OP.add)
        gather("s", ("ph", 0, 2048), ("ptb", 0, 4096), ("el", 0, 128))
        for kk in range(4):
            ts(("pt1", kk, 512, 4), ("pu", 0, 128), c1(KK + kk), OP.mult, c1(A16), OP.add)
        for mr in (0, 1):
            o = mr * 128
            tt(("dz", o + 1, o + 128), (zz, o + 1, o + 128), (zz, o, o + 127), OP.subtract)
        ts(("el", 128, 256), (pe[1], 0, 128), 15.0, OP.add)
        gather("s", ("ph", 2048, 2816), ("ptb", 0, 4096), ("el", 128, 176))
        tt(("hi", 0, 512), ("pt1", 0, 512), ("i61", 0, 512), OP.add)
        cp(("dz", 0, 256, 32), (zz, 0, 256, 32))
        ts(("hi", 0, 512), ("hi", 0, 512), 4, OP.arith_shift_right, 4095, OP.bitwise_and)
        if t == 0: cp(("lu", 0, 768), ("lmb", 256, 1024))
        cp(("hl", 0, 512), ("hi", 0, 512))
        gather("v", ("ph", 2816, 4096), ("ptb", 0, 4096), ("el", 176, 256))
        if t > 0: inverse_list("pt1", "wm", 8192)
        gather("s", ("net", 16, 16 + 1024), ("ph", 0, 4096), ("hl", 0, 64))
        gather("v", ("net", 16 + 1024, AW), ("ph", 0, 4096), ("hl", 64, 128))
        for c in range(1, 4):
            if c == 2: act(("nzt", 0, 256), ("pu", 128, 384), scale=-1.0)
            gather("s", ("net", c * AW + 16, (c + 1) * AW), ("ph", 0, 4096), ("hl", c * 128, (c + 1) * 128))

        def shift(c): cp(("sh%d" % (c % 2), 0, CH), ("net", c * AW + 15, c * AW + 15 + CH))

        def begin(c, mr):
            tt(("sh%d" % (c % 2), 0, CH, 64), ("net", c * AW + 15, c * AW + 15 + CH, 64), ("dz", mr * 128 + c * 32, mr * 128 + c * 32 + 32), OP.add)

        def vv(c, mr): return ("v%d" % mr, c * CH, (c + 1) * CH)

        def differ(c, mr): scan(vv(c, mr), ("net", c * AW + 16, (c + 1) * AW), ("sh%d" % (c % 2), 0, CH), -OFF, OP.add, OP.subtract)

        def hits(c, mr):
            ts(vv(c, mr), vv(c, mr), -OFF, OP.is_equal)
            for s in range(4):
                k = 4 * c + s
                mm((cnt[mr], 0, 512), ("cb", k * 128, (k + 1) * 128), ("v%d" % mr, c * CH + s * 512, c * CH + (s + 1) * 512), k == 0, k == 15)

        shift(0); begin(0, 0); differ(0, 0)
        for c in range(3):
            begin(c, 1)
            if c < 2: shift(c + 1)
            differ(c, 1)
            if c < 2: begin(c + 1, 0)
            hits(c, 0)
            if c < 2: differ(c + 1, 0)
            hits(c, 1)
            if c == 0:
                n = 0
                for mr in (0, 1):
                    for s in range(4):
                        bank = "pcs" if n % 2 == 0 else "pex"
                        n += 1
                        mm((bank, 0, 512), ("idn", 0, 128), ("net", 3 * AW + 16 + s * 512, 3 * AW + 16 + (s + 1) * 512), True, False)
                        mm((bank, 0, 512), ("nzt", mr * 128, mr * 128 + 128), ("xm", s * 512, (s + 1) * 512), False, True)
                        act(("v%d" % mr, 3 * CH + s * 512, 3 * CH + (s + 1) * 512), (bank, 0, 512), bias=-OFF)
        if t == 0:
            for a in range(16):
                act(("rb", a * 128, (a + 1) * 128), ("bd", 0, 128), scale=("dmk", a, a + 1))
        if t < 2: inverse(1 if t == 0 else 3, 0)
        hits(3, 0)
        hits(3, 1)
        if t == 0:
            fill(("mxm", 0, CH, 64), -512.0)
            fill(("mnm", 0, CH, 64), 512.0)
            ts(("pidx", 3, 4), ("pidx", 0, 1), 7, OP.bitwise_and)
            ts(("mc", 0, 256), ("q", 0, 256), c1(PM), OP.is_equal)
            ts(c1(P64), ("pidx", 3, 4), 64.0, OP.mult)
        else: inverse_done(t + 1, "pt1")
        for b in (0, 1):
            o = b * 128
            cp(("lf", o, o + 128), ("lmb", t * 256 + b, (t + 1) * 256, 2))
        if t == 0: ts(("cl", 0, 16), ("clf", 0, 16), c1(P64), OP.add)
        for b in (0, 1):
            o = b * 128
            tt(("ldiff", o, o + 128), ("lmb", (t + 1) * 256 + b, (t + 2) * 256, 2), ("lf", o, o + 128), OP.subtract)

        def extreme(c, which):
            src = ("net", c * AW + 16, (c + 1) * AW)
            if which == 0: scan(vv(c, 0), ("mxm", 0, CH), src, 0.0, OP.add, OP.max)
            else: scan(vv(c, 1), ("mnm", 0, CH), src, 0.0, OP.add, OP.min)

        extreme(0, 0)
        for mr in (0, 1):
            scan(("cm", mr * 512, mr * 512 + 512), ("mxm", 0, 512), (cnt[mr], 0, 512), 0.0, OP.add, OP.max)
        do("v", lambda q: q.tensor_tensor(out=T.cx[:, 0:256], in0=T.cm[:, 0:1024].indirect(T.cl[:, 0:16]), in1=T.mc[:, 0:256], op=OP.mult),
           [("cm", 0, 1024), ("cl", 0, 16), ("mc", 0, 256)], [("cx", 0, 256)])
        for k in range(3):
            o = 0 if k < 2 else 128
            mm(("pc", k * 128, k * 128 + 128), ("bd", 0, 128), ("cx", o, o + 128))
        ts(("m", 0, 256), ("pc", 0, 256), 12.0, OP.is_ge)
        tt(("t0", 0, 256), ("m", 0, 256), ("ldiff", 0, 256), OP.mult)
        tt(("slf", 0, 256), ("t0", 0, 256), ("lf", 0, 256), OP.add)
        cp(("so", 0, 256), ("slf", 0, 256))
        for b in (0, 1):
            gather("s", ("gg", b * 2048, b * 2048 + 2048), ("wr", 0, 4096), ("so", b * 128, b * 128 + 128))
        if t == 0:
            inverse(1, 1)
            inverse_rows("ph", 0)
            inverse(2, 0)
            inverse(2, 1)
        ts(("h1", 0, 128), ("pc", 256, 384), 12.0, OP.is_ge)
        if t == 0: ts(("bm", 0, 256), ("m", 0, 256), 4096.0, OP.mult, 8192.0, OP.add)
        else: ts(("selz", 0, 128), ("m", 0, 128), -1.0, OP.mult, 1.0, OP.add)
        tt(("hh", 0, 128), ("h1", 0, 128), ("m", 0, 128), OP.mult)
        if t == 0:
            ts(("selz", 0, 128), ("m", 0, 128), -1.0, OP.mult, 1.0, OP.add)
            tt(("bm", 0, 256), ("bm", 0, 256), ("slf", 0, 256), OP.add)
        ts(("pen", 0, 128), ("hh", 0, 128), 256.0, OP.mult)
        tt(("selz", 128, 256), ("m", 0, 128), ("hh", 0, 128), OP.subtract)
        red(("tc", 2, 3), ("hh", 0, 128))
        mm(("pt1", 0, 128), ("bd", 0, 128), ("pen", 0, 128), True, False)
        for b in range(32):
            o = (b // 16) * 2048
            mm(("pt1", 0, 128), ("bd", 0, 128), ("gg", o + b % 16, o + 2048, 16), False, b == 31)
        if t == 0: inverse_list("pex", "ph", 0)
        extreme(0, 1)
        for c in range(1, 4):
            extreme(c, 0)
            extreme(c, 1)

        def centres():
            tt(("ys", 0, 128), ("v0", 63, 8192, 64), ("v1", 63, 8192, 64), OP.add)
            for o in (0, 128):
                ts(("y2", o, o + 128), ("ys", 0, 128), 0.5, OP.mult, -0.25, OP.add)
            tt(("q", 0, 256), ("y2", 0, 256), (zz, 0, 256), OP.add)
            ts(("qi", 0, 256), ("q", 0, 256), 0.5, OP.mult, -0.25, OP.add)
            tt(("q", 0, 256), ("qi", 0, 256), (zz, 0, 256), OP.subtract)
            tt(("q", 0, 256), ("q", 0, 256), ("selz", 0, 256), OP.mult)
            tt((zn, 0, 256), ("q", 0, 256), (zz, 0, 256), OP.add)
            owner = rank + 1 + t
            if t < 2:
                send(rank - 1, zn, 128, 256, "zz%d" % (t + 1), 0, "ac%d" % (t + 1))
                send(owner, zn, 0, 128, "zf", t * 128, "af%d" % t)
                arrives(rank + 1, "zz%d" % (t + 1), 0, 128, "ac%d" % (t + 1))
                arrives(rank - 1 - t, "zf", t * 128, t * 128 + 128, "af%d" % t)
            else:
                send(owner, zn, 0, 256, "zf", 256, "af2")
                arrives(rank - 1 - t, "zf", 256, 512, "af2")

        if t == 0:
            ts(("mk8", 0, 128), ("pt1", 0, 128), 768.0, OP.is_lt, -8192.0, OP.mult)
            for o in (0, 128):
                tt(("bm", o, o + 128), ("bm", o, o + 128), ("mk8", 0, 128), OP.add)
            cp(("mo", 0, 256), ("bm", 0, 256))
            scatter(("wm", 0, 16384), ("mo", 0, 256), ("gg", 0, 4096))
            n = 0
            for reg in (0, 4096):
                for a in range(16):
                    mm(("pe0", 0, 256), ("cb", a * 128, (a + 1) * 128), ("wm", reg + a, reg + 4096, 16), n == 0, n == 31)
                    n += 1
        else:
            if t == 2: centres()
            ts(("mk8", 0, 128), ("pt1", 0, 128), 768.0, OP.is_lt, -8192.0, OP.mult)
            for o in (0, 128):
                tt(("mw", o, o + 128), ("mk8", 0, 128), ("selz", o, o + 128), OP.mult)

            def member(e, m, lo, hi):
                r = (t - 1 + m) * 256
                gather(e, ("wm", m * 4096 + lo, m * 4096 + hi), ("mw", m * 128, m * 128 + 128), ("rl", r + lo // 16, r + hi // 16))

            for hf in (0, 1):
                lo, hi = hf * 2048, hf * 2048 + 2048
                cut = hi - 1024 if hf == 1 and t == 1 else hi
                member("s", 0, lo, hi)
                member("v", 1, lo, cut)
                if cut < hi: member("s", 1, cut, hi)
                n = 0
                for reg in (0, 4096):
                    for a in range(16):
                        o = reg + lo
                        mm(("pe0", hf * 128, hf * 128 + 128), ("cb", a * 128, (a + 1) * 128), ("wm", o + a, o + 2048, 16), n == 0, n == 31)
                        n += 1
        if t < 2: centres()
        if t == 0: inverse_done(1, "pex")
        if t == 1: inverse(3, 1)
        red(("tc", 3, 4), ("mk8", 0, 128))
        ts(("tc", 4, 5), ("tc", 3, 4), 1.0 / 8192, OP.mult, 128.0, OP.add)
        tt(("ab", t, t + 1), ("tc", 4, 5), ("tc", 2, 3), OP.subtract)
        if t < 2: ts(c1(A16), ("ab", t, t + 1), 16.0, OP.mult)
        if t == 0: ts(("t0", 0, 256), ("pe0", 0, 256), 1.0, OP.min, 1.0, OP.add)
        else: ts(("t0", 0, 256), ("pe0", 0, 256), 0.0, OP.is_lt, 1.0, OP.add)
        tt(("t0", 0, 256), ("t0", 0, 256), ("wl", 0, 256), OP.mult)
        ts(("w1", 0, 256), ("t0", 0, 256), 8.0, OP.min)
        mm(("pcs", 0, 256), ("bd", 0, 128), ("w1", 0, 256))
        red(("tc", 5, 6), ("pcs", 0, 256))
        ts(("tc", 6, 7), ("tc", 5, 6), 7168.0, OP.is_le, 0.5, OP.max)
        ts(("tc", 7, 8), ("tc", 5, 6), 7168.0, OP.is_gt, 0.25, OP.mult)
        ts(("wi", 0, 256), ("w1", 0, 256), ("tc", 6, 7), OP.mult, ("tc", 7, 8), OP.add)
        cp(("wl", 0, 256), ("wi", 0, 256))

    dma("y", T.ya[:, :], T.ab[0:128:16, 0:3], [("ab", 0, 3)], [])
    dma("s", T.yz[:, 0:256], T.zf[:, 0:256], [("zf", 0, 256)], [])
    for a in range(16):
        pb = ["cnt0", "cnt1", "pex", "pu"][a % 4]
        mm((pb, 0, 256), ("rb", a * 128, (a + 1) * 128), ("wl", 0, 256))
        if a % 2: act(("big", a, 4096, 16), (pb, 0, 256))
        else: cp(("big", a, 4096, 16), (pb, 0, 256))
    dma("y", T.yw[:, :], T.big[0:128:16, 0:4096], [("big", 0, 4096)], [])
    dma("s", T.yz[:, 256:512], T.zf[:, 256:512], [("zf", 256, 512)], [])
    for s, v in total.items():
        if known["g"].get(s, 0) < v: g.wait_ge(T.sem[s], v)
